import numpy as np
import ml_dtypes


def mxq(x, axis, fmt="e4m3"):
    dtype, down = {"e4m3": (ml_dtypes.float8_e4m3fn, 7), "e5m2": (ml_dtypes.float8_e5m2, 14)}[fmt]
    v = np.moveaxis(np.asarray(x, np.float32).astype(ml_dtypes.bfloat16).astype(np.float64), axis, -1)
    blocks = v.reshape(v.shape[:-1] + (-1, 32))
    amax = np.abs(blocks).max(-1, keepdims=True)
    byte = np.maximum(np.where(amax > 0, np.frexp(amax)[1] - 1 + 127, 0) - down, 1)
    scale = np.exp2(byte - 127.0)
    codes = (blocks / scale).astype(np.float32).astype(dtype).astype(np.float64)
    return np.moveaxis((codes * scale).reshape(v.shape), -1, axis)


WIDE = False


def mx_kscale(k):
    if not WIDE:
        return np.ones(k)
    levels = np.array([10, -10, 5, -5, 0])
    if k % 512:
        return np.exp2(np.random.permutation(np.resize(levels, k // 32))).repeat(32)
    a = np.empty((k // 512, 16))
    for p in range(k // 512):
        a[p, :8] = np.random.permutation(np.resize(levels, 8))
        for g in range(8):
            far = levels[np.abs(levels - a[p, g]) >= 10]
            a[p, g + 8] = far[np.random.randint(len(far))]
    return np.exp2(a.ravel()).repeat(32)


def f64(x):
    return np.asarray(x).astype(np.float64)


def striped(idx):
    return np.tile(idx.reshape(-1, 16).T, (8, 1)).astype(np.uint16)


def unstriped(offs):
    return offs[:16].T.reshape(-1).astype(np.int64)


def relu2(v):
    return np.maximum(v, 0.0) ** 2


K, T, D, S, V, N = 2048, 1024, 4, 1024, 256, 128


def setup_inputs():
    n = np.random.standard_normal
    s = mx_kscale(K)[:, None]
    return {
        "xT": (n((K, T)) * s).astype(np.float32),
        "w": (n((D, K, N)) / np.sqrt(D * K) / s[None]).astype(np.float32),
        "b": (0.3 * n((N, 1))).astype(np.float32),
        "gate": np.tile(np.random.uniform(0.2, 1.0, S), (N, 1)).astype(np.float32),
        "offs": striped(np.random.permutation(T)[:S]),
    }


def reference(xT, w, b, gate, offs):
    idx = unstriped(offs)
    xq = mxq(f64(xT)[:, idx], 0, "e4m3")
    wq = mxq(f64(w), 1, "e4m3")
    y = sum(wq[d].T @ xq[:, d * V:(d + 1) * V] for d in range(D))
    y = relu2(y + f64(b))
    out = np.zeros((N, T))
    out[:, idx] = f64(gate) * np.tile(y, (1, D))
    return out

@@ -1,0 +1,192 @@
+from contextlib import ExitStack
+
+import concourse.mybir as mybir
+
+K, T, D, S, V, N = 2048, 1024, 4, 1024, 256, 128
+FLOPS = 2 * N * S * K
+
+F32 = mybir.dt.float32
+BF16 = mybir.dt.bfloat16
+U32 = mybir.dt.uint32
+U16 = mybir.dt.uint16
+U8 = mybir.dt.uint8
+FP8X4 = mybir.dt.float8_e4m3fn_x4
+ACT = mybir.ActivationFunctionType
+ALU = mybir.AluOpType
+
+P = 128
+PACK = 4
+PASS_K = P * PACK
+PASSES = K // PASS_K
+HALF = T // 2
+X_WINDOW = 1408
+OUT_WINDOW = 2048
+VH = V // 2
+
+X_VECTOR = ((256, 320), (64, 384), (192, 128), (0, 128))
+W_ENGINES = ("VSSS", "SSSS", "SSVS", "SSBB")
+X_SPLIT = ((1024,), (1024,), (1024,), (512, 512))
+W3_GROUPS = [(0, 1), (2,), (3,)]
+
+
+def tile_picked_tome_lin_relu2_sub_e_kernel(tc, xT, w, b, gate, offs, out):
+    nc = tc.nc
+    with ExitStack() as ctx:
+        keep = ctx.enter_context(tc.tile_pool(name="keep", bufs=1))
+        psum = ctx.enter_context(tc.psum_pool(name="psum", bufs=1))
+
+        offsets = keep.tile([P, S // 16], U16, name="offsets")
+        bias = keep.tile([P, 1], F32, name="bias")
+        gates = keep.tile([P, S], F32, name="gates")
+        x_raw = [[keep.tile([P, PACK, n], F32, name=f"x_raw{a}_{i}") for i, n in enumerate(X_SPLIT[a])] for a in range(PASSES)]
+        w_groups = [[(0, 1, 2, 3)]] * 3 + [W3_GROUPS]
+        w_raw = [[keep.tile([P, len(g), PACK, N], F32, name=f"w_raw{a}_{i}") for i, g in enumerate(w_groups[a])] for a in range(PASSES)]
+        x_bf = [[keep.tile([P, HALF, PACK], BF16, name=f"x_bf{a}_{c}", align_bytes=64) for c in range(2)] for a in range(PASSES)]
+        w_bf = [keep.tile([P, D, N, PACK], BF16, name=f"w_bf{a}", tag=f"ring{a}", align_bytes=64) for a in range(PASSES)]
+        x_codes = [keep.tile([P, X_WINDOW], U32, name=f"x_codes{a}", align_bytes=64) for a in range(PASSES)]
+        x_scales = keep.tile([P, X_WINDOW], U8, name="x_scales", align_bytes=64)
+        picked_codes = [keep.tile([P, S], U32, name=f"picked_codes{a}", align_bytes=64) for a in range(PASSES - 1)]
+        picked_scales = keep.tile([P, S], U8, name="picked_scales", align_bytes=64)
+        w_codes = [keep.tile([P, D * N], U32, name=f"w_codes{a}", align_bytes=64) for a in range(PASSES)]
+        w_scales = [keep.tile([P, D * N], U8, name=f"w_scales{a}", align_bytes=64) for a in range(PASSES)]
+        r = keep.tile([P, V], F32, name="r")
+        ug = keep.tile([P, V], F32, name="ug")
+        y = keep.tile([P, D - 1, V], F32, name="y")
+        result = keep.tile([P, OUT_WINDOW], F32, name="result")
+        acc = [psum.tile([P, VH], F32, name=f"acc{h}") for h in range(2)]
+
+        nc.scalar.dma_start(out=bias[:], in_=b)
+        for a in range(PASSES):
+            t0 = 0
+            for i, n in enumerate(X_SPLIT[a]):
+                src = xT[a * PASS_K : (a + 1) * PASS_K, t0 : t0 + n]
+                nc.sync.dma_start(out=x_raw[a][i][:], in_=src.rearrange("(p j) t -> p j t", j=PACK))
+                t0 += n
+            if a == 0:
+                nc.sync.dma_start(offsets[:], offs)
+        for a in range(PASSES):
+            for i, g in enumerate(w_groups[a]):
+                src = w[g[0] : g[-1] + 1, a * PASS_K : (a + 1) * PASS_K, :].rearrange("d (p j) m -> p d j m", j=PACK)
+                nc.sync.dma_start(out=w_raw[a][i][:], in_=src)
+        nc.sync.dma_start(out=gates[:], in_=gate)
+
+        nc.gpsimd.memset(x_scales[:], 0)
+        for a in range(PASSES):
+            nc.gpsimd.memset(x_codes[a][:, T:X_WINDOW], 0)
+
+        def interleave(engine, dst, src):
+            o = dst.rearrange("p (c i) j -> p c j i", i=4)
+            s = src.rearrange("p j (c i) -> p c j i", i=4)
+            if engine == "V":
+                nc.vector.tensor_copy(out=o, in_=s)
+            else:
+                nc.scalar.copy(out=o, in_=s)
+
+        def x_columns(a, lo, hi):
+            t0 = 0
+            for i, n in enumerate(X_SPLIT[a]):
+                if t0 <= lo and hi <= t0 + n:
+                    return x_raw[a][i][:, :, lo - t0 : hi - t0]
+                t0 += n
+
+        def convert_x(a, c):
+            lo, mid, hi = c * HALF, (c + 1) * HALF - X_VECTOR[a][c], (c + 1) * HALF
+            if mid > lo:
+                interleave("S", x_bf[a][c][:, 0 : mid - lo, :], x_columns(a, lo, mid))
+            if hi > mid:
+                interleave("V", x_bf[a][c][:, mid - lo : HALF, :], x_columns(a, mid, hi))
+
+        def quantize_x(a, c):
+            cols = slice(c * HALF, (c + 1) * HALF)
+            nc.vector.quantize_mx(
+                out=x_codes[a][:, cols].bitcast(FP8X4),
+                scales=x_scales[4 * a : P, cols],
+                in_=x_bf[a][c][:].rearrange("p t j -> p (t j)"),
+            )
+
+        def convert_w(a, i):
+            for n, d in enumerate(w_groups[a][i]):
+                e = W_ENGINES[a][d]
+                if e == "B":
+                    interleave("S", w_bf[a][:, d, 0 : N // 2, :], w_raw[a][i][:, n, :, 0 : N // 2])
+                    interleave("V", w_bf[a][:, d, N // 2 : N, :], w_raw[a][i][:, n, :, N // 2 : N])
+                else:
+                    interleave(e, w_bf[a][:, d, :, :], w_raw[a][i][:, n, :, :])
+
+        def quantize_w(a, i):
+            g = w_groups[a][i]
+            cols = slice(g[0] * N, (g[-1] + 1) * N)
+            nc.vector.quantize_mx(
+                out=w_codes[a][:, cols].bitcast(FP8X4),
+                scales=w_scales[a][:, cols],
+                in_=w_bf[a][:, g[0] : g[-1] + 1, :, :].rearrange("p d m j -> p (d m j)"),
+            )
+
+        def gather(dst, src, lo, hi):
+            nc.vector.tensor_copy(dst, src[:].indirect(offsets[:, lo // 16 : hi // 16]))
+
+        def multiply(a, d):
+            for h in range(2):
+                cols = slice(d * V + h * VH, d * V + (h + 1) * VH)
+                if a < PASSES - 1:
+                    codes = picked_codes[a][:, cols]
+                else:
+                    codes = last_codes[d // 2][:, cols.start % (S // 2) : cols.start % (S // 2) + VH]
+                nc.tensor.matmul_mx(
+                    out=acc[h][:],
+                    lhsT=w_codes[a][:, d * N : (d + 1) * N].bitcast(FP8X4),
+                    lhsT_scale=w_scales[a][:, d * N : (d + 1) * N],
+                    rhs=codes.bitcast(FP8X4),
+                    rhs_scale=picked_scales[4 * a : P, cols],
+                    start=(a == 0 and d == 0),
+                    stop=(a == PASSES - 1 and d == D - 1),
+                )
+
+        def weights(a, i):
+            convert_w(a, i)
+            quantize_w(a, i)
+
+        for a in range(PASSES):
+            for c in range(2):
+                convert_x(a, c)
+            for c in range(2):
+                quantize_x(a, c)
+            if a < PASSES - 1:
+                gather(picked_codes[a][:], x_codes[a], 0, S)
+        gather(picked_scales[:, 0 : S // 2], x_scales, 0, S // 2)
+        weights(0, 0)
+        gather(picked_scales[:, S // 2 : S], x_scales, S // 2, S)
+        for d in (0, 1):
+            multiply(0, d)
+        last_codes = []
+        last_codes.append(keep.tile([P, S // 2], U32, name="last_codes0", tag="ring0", align_bytes=64))
+        gather(last_codes[0][:], x_codes[3], 0, S // 2)
+        weights(1, 0)
+        for d in (0, 1):
+            multiply(1, d)
+        for a in (0, 1):
+            for d in (2, 3):
+                multiply(a, d)
+        last_codes.append(keep.tile([P, S // 2], U32, name="last_codes1", tag="ring1", align_bytes=64))
+        gather(last_codes[1][:], x_codes[3], S // 2, S)
+        weights(2, 0)
+        for d in range(D):
+            multiply(2, d)
+        for i, g in enumerate(W3_GROUPS):
+            weights(3, i)
+            for d in g:
+                multiply(3, d)
+
+        halves = [slice(0, VH), slice(VH, V)]
+        for h in (0, 1):
+            nc.scalar.activation(out=r[:, halves[h]], in_=acc[h][:], func=ACT.Relu, bias=bias[:, 0:1])
+        for h in (1, 0):
+            nc.vector.scalar_tensor_tensor(
+                out=ug[:, halves[h]], in0=acc[h][:], scalar=bias[:, 0:1], in1=gates[:, halves[h]], op0=ALU.add, op1=ALU.mult
+            )
+        nc.scalar.activation(out=y[:], in_=r[:].unsqueeze(1).to_broadcast([P, D - 1, V]), func=ACT.Square)
+        nc.vector.tensor_tensor(result[:].indirect(offsets[:, 0 : V // 16]), r[:], ug[:], ALU.mult)
+        nc.vector.tensor_tensor(
+            result[:].indirect(offsets[:, V // 16 : S // 16]), y[:].rearrange("p d v -> p (d v)"), gates[:, V:S], ALU.mult
+        )
+        nc.sync.dma_start(out=out, in_=result[:, 0:T])

@@ -23,10 +23,10 @@ X_WINDOW = 1408
 OUT_WINDOW = 2048
 VH = V // 2
 
-X_VECTOR = ((256, 320), (64, 384), (192, 128), (0, 128))
-W_ENGINES = ("VSSS", "SSSS", "SSVS", "SSBB")
+X_VECTOR = ((320, 320), (192, 256), (192, 256), (0, 256))
+W_ENGINES = ("SSSS", "SSSS", "SSSS", "SSSB")
 X_SPLIT = ((1024,), (1024,), (1024,), (512, 512))
-W3_GROUPS = [(0, 1), (2,), (3,)]
+W_GROUPS = ([(0, 1, 2, 3)], [(0, 1, 2, 3)], [(0, 1), (2, 3)], [(0, 1), (2,), (3,)])
 
 
 def tile_picked_tome_lin_relu2_sub_e_kernel(tc, xT, w, b, gate, offs, out):
@@ -39,8 +39,8 @@ def tile_picked_tome_lin_relu2_sub_e_kernel(tc, xT, w, b, gate, offs, out):
         bias = keep.tile([P, 1], F32, name="bias")
         gates = keep.tile([P, S], F32, name="gates")
         x_raw = [[keep.tile([P, PACK, n], F32, name=f"x_raw{a}_{i}") for i, n in enumerate(X_SPLIT[a])] for a in range(PASSES)]
-        w_groups = [[(0, 1, 2, 3)]] * 3 + [W3_GROUPS]
-        w_raw = [[keep.tile([P, len(g), PACK, N], F32, name=f"w_raw{a}_{i}") for i, g in enumerate(w_groups[a])] for a in range(PASSES)]
+        w_groups = W_GROUPS
+        w_raw = [[keep.tile([P, PACK, N], F32, name=f"w_raw{a}_{d}") for d in range(D)] for a in range(PASSES)]
         x_bf = [[keep.tile([P, HALF, PACK], BF16, name=f"x_bf{a}_{c}", align_bytes=64) for c in range(2)] for a in range(PASSES)]
         w_bf = [keep.tile([P, D, N, PACK], BF16, name=f"w_bf{a}", tag=f"ring{a}", align_bytes=64) for a in range(PASSES)]
         x_codes = [keep.tile([P, X_WINDOW], U32, name=f"x_codes{a}", align_bytes=64) for a in range(PASSES)]
@@ -55,7 +55,6 @@ def tile_picked_tome_lin_relu2_sub_e_kernel(tc, xT, w, b, gate, offs, out):
         result = keep.tile([P, OUT_WINDOW], F32, name="result")
         acc = [psum.tile([P, VH], F32, name=f"acc{h}") for h in range(2)]
 
-        nc.scalar.dma_start(out=bias[:], in_=b)
         for a in range(PASSES):
             t0 = 0
             for i, n in enumerate(X_SPLIT[a]):
@@ -65,10 +64,12 @@ def tile_picked_tome_lin_relu2_sub_e_kernel(tc, xT, w, b, gate, offs, out):
             if a == 0:
                 nc.sync.dma_start(offsets[:], offs)
         for a in range(PASSES):
-            for i, g in enumerate(w_groups[a]):
-                src = w[g[0] : g[-1] + 1, a * PASS_K : (a + 1) * PASS_K, :].rearrange("d (p j) m -> p d j m", j=PACK)
-                nc.sync.dma_start(out=w_raw[a][i][:], in_=src)
-        nc.sync.dma_start(out=gates[:], in_=gate)
+            for d in range(D):
+                src = w[d, a * PASS_K : (a + 1) * PASS_K, :].rearrange("(p j) m -> p j m", j=PACK)
+                nc.sync.dma_start(out=w_raw[a][d][:], in_=src)
+        nc.sync.dma_start(out=bias[:], in_=b)
+        nc.sync.dma_start(out=gates[:, 0:V], in_=gate[:, 0:V])
+        nc.sync.dma_start(out=gates[:, V:S], in_=gate[:, V:S])
 
         nc.gpsimd.memset(x_scales[:], 0)
         for a in range(PASSES):
@@ -105,13 +106,13 @@ def tile_picked_tome_lin_relu2_sub_e_kernel(tc, xT, w, b, gate, offs, out):
             )
 
         def convert_w(a, i):
-            for n, d in enumerate(w_groups[a][i]):
+            for d in w_groups[a][i]:
                 e = W_ENGINES[a][d]
                 if e == "B":
-                    interleave("S", w_bf[a][:, d, 0 : N // 2, :], w_raw[a][i][:, n, :, 0 : N // 2])
-                    interleave("V", w_bf[a][:, d, N // 2 : N, :], w_raw[a][i][:, n, :, N // 2 : N])
+                    interleave("S", w_bf[a][:, d, 0 : N // 2, :], w_raw[a][d][:, :, 0 : N // 2])
+                    interleave("V", w_bf[a][:, d, N // 2 : N, :], w_raw[a][d][:, :, N // 2 : N])
                 else:
-                    interleave(e, w_bf[a][:, d, :, :], w_raw[a][i][:, n, :, :])
+                    interleave(e, w_bf[a][:, d, :, :], w_raw[a][d][:])
 
         def quantize_w(a, i):
             g = w_groups[a][i]
@@ -169,13 +170,11 @@ def tile_picked_tome_lin_relu2_sub_e_kernel(tc, xT, w, b, gate, offs, out):
                 multiply(a, d)
         last_codes.append(keep.tile([P, S // 2], U32, name="last_codes1", tag="ring1", align_bytes=64))
         gather(last_codes[1][:], x_codes[3], S // 2, S)
-        weights(2, 0)
-        for d in range(D):
-            multiply(2, d)
-        for i, g in enumerate(W3_GROUPS):
-            weights(3, i)
-            for d in g:
-                multiply(3, d)
+        for a in (2, 3):
+            for i, g in enumerate(w_groups[a]):
+                weights(a, i)
+                for d in g:
+                    multiply(a, d)
 
         halves = [slice(0, VH), slice(VH, V)]
         for h in (0, 1):

@@ -23,8 +23,9 @@ X_WINDOW = 1408
 OUT_WINDOW = 2048
 VH = V // 2
 
-X_VECTOR = ((320, 320), (192, 256), (192, 256), (0, 256))
-W_ENGINES = ("SSSS", "SSSS", "SSSS", "SSSB")
+X_VECTOR = ((320, 320), (256, 256), (256, 256), (0, 384))
+W_ENGINES = ("SSSS", "SSSS", "SSSV", "SSSB")
+W_LOADS = ([(0, 1), (2, 3)], [(0, 1), (2, 3)], [(0, 1), (2, 3)], [(0, 1), (2,), (3,)])
 X_SPLIT = ((1024,), (1024,), (1024,), (512, 512))
 W_GROUPS = ([(0, 1, 2, 3)], [(0, 1, 2, 3)], [(0, 1), (2, 3)], [(0, 1), (2,), (3,)])
 
@@ -40,7 +41,8 @@ def tile_picked_tome_lin_relu2_sub_e_kernel(tc, xT, w, b, gate, offs, out):
         gates = keep.tile([P, S], F32, name="gates")
         x_raw = [[keep.tile([P, PACK, n], F32, name=f"x_raw{a}_{i}") for i, n in enumerate(X_SPLIT[a])] for a in range(PASSES)]
         w_groups = W_GROUPS
-        w_raw = [[keep.tile([P, PACK, N], F32, name=f"w_raw{a}_{d}") for d in range(D)] for a in range(PASSES)]
+        w_in = [[keep.tile([P, len(g), PACK, N], F32, name=f"w_in{a}_{i}") for i, g in enumerate(W_LOADS[a])] for a in range(PASSES)]
+        w_raw = [[w_in[a][i][:, n, :, :] for i, g in enumerate(W_LOADS[a]) for n in range(len(g))] for a in range(PASSES)]
         x_bf = [[keep.tile([P, HALF, PACK], BF16, name=f"x_bf{a}_{c}", align_bytes=64) for c in range(2)] for a in range(PASSES)]
         w_bf = [keep.tile([P, D, N, PACK], BF16, name=f"w_bf{a}", tag=f"ring{a}", align_bytes=64) for a in range(PASSES)]
         x_codes = [keep.tile([P, X_WINDOW], U32, name=f"x_codes{a}", align_bytes=64) for a in range(PASSES)]
@@ -64,9 +66,9 @@ def tile_picked_tome_lin_relu2_sub_e_kernel(tc, xT, w, b, gate, offs, out):
             if a == 0:
                 nc.sync.dma_start(offsets[:], offs)
         for a in range(PASSES):
-            for d in range(D):
-                src = w[d, a * PASS_K : (a + 1) * PASS_K, :].rearrange("(p j) m -> p j m", j=PACK)
-                nc.sync.dma_start(out=w_raw[a][d][:], in_=src)
+            for i, g in enumerate(W_LOADS[a]):
+                src = w[g[0] : g[-1] + 1, a * PASS_K : (a + 1) * PASS_K, :].rearrange("d (p j) m -> p d j m", j=PACK)
+                nc.sync.dma_start(out=w_in[a][i][:], in_=src)
         nc.sync.dma_start(out=bias[:], in_=b)
         nc.sync.dma_start(out=gates[:, 0:V], in_=gate[:, 0:V])
         nc.sync.dma_start(out=gates[:, V:S], in_=gate[:, V:S])
@@ -112,7 +114,7 @@ def tile_picked_tome_lin_relu2_sub_e_kernel(tc, xT, w, b, gate, offs, out):
                     interleave("S", w_bf[a][:, d, 0 : N // 2, :], w_raw[a][d][:, :, 0 : N // 2])
                     interleave("V", w_bf[a][:, d, N // 2 : N, :], w_raw[a][d][:, :, N // 2 : N])
                 else:
-                    interleave(e, w_bf[a][:, d, :, :], w_raw[a][d][:])
+                    interleave(e, w_bf[a][:, d, :, :], w_raw[a][d])
 
         def quantize_w(a, i):
             g = w_groups[a][i]

@@ -18,16 +18,18 @@ P = 128
 PACK = 4
 PASS_K = P * PACK
 PASSES = K // PASS_K
+LAST = PASSES - 1
 HALF = T // 2
 X_WINDOW = 1408
 OUT_WINDOW = 2048
 VH = V // 2
+RUN = 4
 
-X_VECTOR = ((320, 320), (256, 256), (256, 256), (0, 384))
-W_ENGINES = ("SSSS", "SSSS", "SSSV", "SSSB")
-W_LOADS = ([(0, 1), (2, 3)], [(0, 1), (2, 3)], [(0, 1), (2, 3)], [(0, 1), (2,), (3,)])
+X_VECTOR = ((320, 320), (128, 256), (128, 256), (0, 128))
 X_SPLIT = ((1024,), (1024,), (1024,), (512, 512))
-W_GROUPS = ([(0, 1, 2, 3)], [(0, 1, 2, 3)], [(0, 1), (2, 3)], [(0, 1), (2,), (3,)])
+W_VECTOR = ((0, 0, 0, 0), (0, 0, 0, 0), (0, 0, 0, 0), (0, 0, 0, 64))
+W_LOADS = ([(0, 1), (2, 3)], [(0, 1), (2, 3)], [(0, 1), (2, 3)], [(0, 1), (2,), (3,)])
+W_GROUPS = ([(0, 1, 2, 3)], [(0, 1), (2, 3)], [(0, 1), (2, 3)], [(0, 1), (2,), (3,)])
 
 
 def tile_picked_tome_lin_relu2_sub_e_kernel(tc, xT, w, b, gate, offs, out):
@@ -39,15 +41,16 @@ def tile_picked_tome_lin_relu2_sub_e_kernel(tc, xT, w, b, gate, offs, out):
         offsets = keep.tile([P, S // 16], U16, name="offsets")
         bias = keep.tile([P, 1], F32, name="bias")
         gates = keep.tile([P, S], F32, name="gates")
-        x_raw = [[keep.tile([P, PACK, n], F32, name=f"x_raw{a}_{i}") for i, n in enumerate(X_SPLIT[a])] for a in range(PASSES)]
-        w_groups = W_GROUPS
-        w_in = [[keep.tile([P, len(g), PACK, N], F32, name=f"w_in{a}_{i}") for i, g in enumerate(W_LOADS[a])] for a in range(PASSES)]
+        x_raw = [[keep.tile([P, PACK, n], F32, name=f"x_raw{a}_{i}", tag=f"x_in{a}_{i}", align_bytes=64) for i, n in enumerate(X_SPLIT[a])] for a in range(PASSES)]
+        w_in = [[keep.tile([P, len(g), PACK, N], F32, name=f"w_in{a}_{i}", tag=f"w_in{a}_{i}", align_bytes=64) for i, g in enumerate(W_LOADS[a])] for a in range(PASSES)]
         w_raw = [[w_in[a][i][:, n, :, :] for i, g in enumerate(W_LOADS[a]) for n in range(len(g))] for a in range(PASSES)]
         x_bf = [[keep.tile([P, HALF, PACK], BF16, name=f"x_bf{a}_{c}", align_bytes=64) for c in range(2)] for a in range(PASSES)]
-        w_bf = [keep.tile([P, D, N, PACK], BF16, name=f"w_bf{a}", tag=f"ring{a}", align_bytes=64) for a in range(PASSES)]
+        w_bf = [
+            [keep.tile([P, len(g), N, PACK], BF16, name=f"w_bf{a}_{i}", tag=(f"w_in{LAST}_1" if (a, i) == (LAST, 2) else f"w_bf{a}_{i}"), align_bytes=64) for i, g in enumerate(W_GROUPS[a])]
+            for a in range(PASSES)
+        ]
         x_codes = [keep.tile([P, X_WINDOW], U32, name=f"x_codes{a}", align_bytes=64) for a in range(PASSES)]
         x_scales = keep.tile([P, X_WINDOW], U8, name="x_scales", align_bytes=64)
-        picked_codes = [keep.tile([P, S], U32, name=f"picked_codes{a}", align_bytes=64) for a in range(PASSES - 1)]
         picked_scales = keep.tile([P, S], U8, name="picked_scales", align_bytes=64)
         w_codes = [keep.tile([P, D * N], U32, name=f"w_codes{a}", align_bytes=64) for a in range(PASSES)]
         w_scales = [keep.tile([P, D * N], U8, name=f"w_scales{a}", align_bytes=64) for a in range(PASSES)]
@@ -57,6 +60,7 @@ def tile_picked_tome_lin_relu2_sub_e_kernel(tc, xT, w, b, gate, offs, out):
         result = keep.tile([P, OUT_WINDOW], F32, name="result")
         acc = [psum.tile([P, VH], F32, name=f"acc{h}") for h in range(2)]
 
+        nc.scalar.dma_start(out=bias[:], in_=b)
         for a in range(PASSES):
             t0 = 0
             for i, n in enumerate(X_SPLIT[a]):
@@ -69,35 +73,26 @@ def tile_picked_tome_lin_relu2_sub_e_kernel(tc, xT, w, b, gate, offs, out):
             for i, g in enumerate(W_LOADS[a]):
                 src = w[g[0] : g[-1] + 1, a * PASS_K : (a + 1) * PASS_K, :].rearrange("d (p j) m -> p d j m", j=PACK)
                 nc.sync.dma_start(out=w_in[a][i][:], in_=src)
-        nc.sync.dma_start(out=bias[:], in_=b)
-        nc.sync.dma_start(out=gates[:, 0:V], in_=gate[:, 0:V])
-        nc.sync.dma_start(out=gates[:, V:S], in_=gate[:, V:S])
+        nc.sync.dma_start(out=gates[:], in_=gate)
 
         nc.gpsimd.memset(x_scales[:], 0)
         for a in range(PASSES):
             nc.gpsimd.memset(x_codes[a][:, T:X_WINDOW], 0)
 
-        def interleave(engine, dst, src):
-            o = dst.rearrange("p (c i) j -> p c j i", i=4)
-            s = src.rearrange("p j (c i) -> p c j i", i=4)
-            if engine == "V":
-                nc.vector.tensor_copy(out=o, in_=s)
-            else:
-                nc.scalar.copy(out=o, in_=s)
+        def interleave(copy, dst, src):
+            copy(out=dst.rearrange("p (c i) j -> p c j i", i=RUN), in_=src.rearrange("p j (c i) -> p c j i", i=RUN))
 
-        def x_columns(a, lo, hi):
-            t0 = 0
-            for i, n in enumerate(X_SPLIT[a]):
-                if t0 <= lo and hi <= t0 + n:
-                    return x_raw[a][i][:, :, lo - t0 : hi - t0]
-                t0 += n
+        def shared_interleave(dst, src, on_vector):
+            mid = dst.shape[1] - on_vector
+            if mid > 0:
+                interleave(nc.scalar.copy, dst[:, 0:mid, :], src[:, :, 0:mid])
+            if on_vector > 0:
+                interleave(nc.vector.tensor_copy, dst[:, mid:, :], src[:, :, mid:])
 
-        def convert_x(a, c):
-            lo, mid, hi = c * HALF, (c + 1) * HALF - X_VECTOR[a][c], (c + 1) * HALF
-            if mid > lo:
-                interleave("S", x_bf[a][c][:, 0 : mid - lo, :], x_columns(a, lo, mid))
-            if hi > mid:
-                interleave("V", x_bf[a][c][:, mid - lo : HALF, :], x_columns(a, mid, hi))
+        def x_half(a, c):
+            if len(X_SPLIT[a]) == 2:
+                return x_raw[a][c][:]
+            return x_raw[a][0][:, :, c * HALF : (c + 1) * HALF]
 
         def quantize_x(a, c):
             cols = slice(c * HALF, (c + 1) * HALF)
@@ -107,74 +102,51 @@ def tile_picked_tome_lin_relu2_sub_e_kernel(tc, xT, w, b, gate, offs, out):
                 in_=x_bf[a][c][:].rearrange("p t j -> p (t j)"),
             )
 
-        def convert_w(a, i):
-            for d in w_groups[a][i]:
-                e = W_ENGINES[a][d]
-                if e == "B":
-                    interleave("S", w_bf[a][:, d, 0 : N // 2, :], w_raw[a][d][:, :, 0 : N // 2])
-                    interleave("V", w_bf[a][:, d, N // 2 : N, :], w_raw[a][d][:, :, N // 2 : N])
-                else:
-                    interleave(e, w_bf[a][:, d, :, :], w_raw[a][d])
-
-        def quantize_w(a, i):
-            g = w_groups[a][i]
+        def weights(a, i):
+            g = W_GROUPS[a][i]
+            for n, d in enumerate(g):
+                shared_interleave(w_bf[a][i][:, n, :, :], w_raw[a][d], W_VECTOR[a][d])
             cols = slice(g[0] * N, (g[-1] + 1) * N)
             nc.vector.quantize_mx(
                 out=w_codes[a][:, cols].bitcast(FP8X4),
                 scales=w_scales[a][:, cols],
-                in_=w_bf[a][:, g[0] : g[-1] + 1, :, :].rearrange("p d m j -> p (d m j)"),
+                in_=w_bf[a][i][:].rearrange("p d m j -> p (d m j)"),
             )
 
-        def gather(dst, src, lo, hi):
-            nc.vector.tensor_copy(dst, src[:].indirect(offsets[:, lo // 16 : hi // 16]))
+        picked = {}
+
+        def gather_codes(a, lo, hi, tag):
+            dst = keep.tile([P, hi - lo], U32, name=f"picked{a}_{lo}", tag=tag, align_bytes=64)
+            nc.vector.tensor_copy(dst[:], x_codes[a][:].indirect(offsets[:, lo // 16 : hi // 16]))
+            for s in range(lo, hi, VH):
+                picked[a, s] = dst[:, s - lo : s - lo + VH]
 
         def multiply(a, d):
             for h in range(2):
-                cols = slice(d * V + h * VH, d * V + (h + 1) * VH)
-                if a < PASSES - 1:
-                    codes = picked_codes[a][:, cols]
-                else:
-                    codes = last_codes[d // 2][:, cols.start % (S // 2) : cols.start % (S // 2) + VH]
+                s = d * V + h * VH
                 nc.tensor.matmul_mx(
                     out=acc[h][:],
                     lhsT=w_codes[a][:, d * N : (d + 1) * N].bitcast(FP8X4),
                     lhsT_scale=w_scales[a][:, d * N : (d + 1) * N],
-                    rhs=codes.bitcast(FP8X4),
-                    rhs_scale=picked_scales[4 * a : P, cols],
+                    rhs=picked[a, s].bitcast(FP8X4),
+                    rhs_scale=picked_scales[4 * a : P, s : s + VH],
                     start=(a == 0 and d == 0),
-                    stop=(a == PASSES - 1 and d == D - 1),
+                    stop=(a == LAST and d == D - 1),
                 )
-
-        def weights(a, i):
-            convert_w(a, i)
-            quantize_w(a, i)
 
         for a in range(PASSES):
             for c in range(2):
-                convert_x(a, c)
+                shared_interleave(x_bf[a][c][:], x_half(a, c), X_VECTOR[a][c])
             for c in range(2):
                 quantize_x(a, c)
-            if a < PASSES - 1:
-                gather(picked_codes[a][:], x_codes[a], 0, S)
-        gather(picked_scales[:, 0 : S // 2], x_scales, 0, S // 2)
-        weights(0, 0)
-        gather(picked_scales[:, S // 2 : S], x_scales, S // 2, S)
-        for d in (0, 1):
-            multiply(0, d)
-        last_codes = []
-        last_codes.append(keep.tile([P, S // 2], U32, name="last_codes0", tag="ring0", align_bytes=64))
-        gather(last_codes[0][:], x_codes[3], 0, S // 2)
-        weights(1, 0)
-        for d in (0, 1):
-            multiply(1, d)
-        for a in (0, 1):
-            for d in (2, 3):
-                multiply(a, d)
-        last_codes.append(keep.tile([P, S // 2], U32, name="last_codes1", tag="ring1", align_bytes=64))
-        gather(last_codes[1][:], x_codes[3], S // 2, S)
-        for a in (2, 3):
-            for i, g in enumerate(w_groups[a]):
+            if a < LAST:
+                gather_codes(a, 0, S, f"head{a}")
+        nc.vector.tensor_copy(picked_scales[:], x_scales[:].indirect(offsets[:]))
+        for a in range(PASSES):
+            for i, g in enumerate(W_GROUPS[a]):
                 weights(a, i)
+                if a in (1, 2) and i == 0:
+                    gather_codes(LAST, (a - 1) * HALF, a * HALF, f"w_in{a}_0")
                 for d in g:
                     multiply(a, d)
 

@@ -23,13 +23,12 @@ HALF = T // 2
 X_WINDOW = 1408
 OUT_WINDOW = 2048
 VH = V // 2
-RUN = 4
+RUN = 2
 
-X_VECTOR = ((320, 320), (128, 256), (128, 256), (0, 128))
+X_VECTOR = ((256, 256), (192, 192), (192, 192), (0, 128))
 X_SPLIT = ((1024,), (1024,), (1024,), (512, 512))
-W_VECTOR = ((0, 0, 0, 0), (0, 0, 0, 0), (0, 0, 0, 0), (0, 0, 0, 64))
-W_LOADS = ([(0, 1), (2, 3)], [(0, 1), (2, 3)], [(0, 1), (2, 3)], [(0, 1), (2,), (3,)])
-W_GROUPS = ([(0, 1, 2, 3)], [(0, 1), (2, 3)], [(0, 1), (2, 3)], [(0, 1), (2,), (3,)])
+W_LOADS = ((0, 0, 4), (1, 0, 4), (2, 0, 4), (3, 0, 2), (3, 2, 3), (3, 3, 4))
+W_VECTOR = (0, 0, 32, 0, 0, 64)
 
 
 def tile_picked_tome_lin_relu2_sub_e_kernel(tc, xT, w, b, gate, offs, out):
@@ -41,14 +40,11 @@ def tile_picked_tome_lin_relu2_sub_e_kernel(tc, xT, w, b, gate, offs, out):
         offsets = keep.tile([P, S // 16], U16, name="offsets")
         bias = keep.tile([P, 1], F32, name="bias")
         gates = keep.tile([P, S], F32, name="gates")
-        x_raw = [[keep.tile([P, PACK, n], F32, name=f"x_raw{a}_{i}", tag=f"x_in{a}_{i}", align_bytes=64) for i, n in enumerate(X_SPLIT[a])] for a in range(PASSES)]
-        w_in = [[keep.tile([P, len(g), PACK, N], F32, name=f"w_in{a}_{i}", tag=f"w_in{a}_{i}", align_bytes=64) for i, g in enumerate(W_LOADS[a])] for a in range(PASSES)]
-        w_raw = [[w_in[a][i][:, n, :, :] for i, g in enumerate(W_LOADS[a]) for n in range(len(g))] for a in range(PASSES)]
-        x_bf = [[keep.tile([P, HALF, PACK], BF16, name=f"x_bf{a}_{c}", align_bytes=64) for c in range(2)] for a in range(PASSES)]
-        w_bf = [
-            [keep.tile([P, len(g), N, PACK], BF16, name=f"w_bf{a}_{i}", tag=(f"w_in{LAST}_1" if (a, i) == (LAST, 2) else f"w_bf{a}_{i}"), align_bytes=64) for i, g in enumerate(W_GROUPS[a])]
-            for a in range(PASSES)
+        x_raw = [[keep.tile([P, PACK, n], F32, name=f"x_raw{a}_{i}") for i, n in enumerate(X_SPLIT[a])] for a in range(PASSES)]
+        w_raw = [
+            keep.tile([P, hi - lo, PACK, N], F32, name=f"w_raw{i}", tag=f"w_slot{i}", align_bytes=64) for i, (a, lo, hi) in enumerate(W_LOADS)
         ]
+        x_bf = [[keep.tile([P, HALF, PACK], BF16, name=f"x_bf{a}_{c}", align_bytes=64) for c in range(2)] for a in range(PASSES)]
         x_codes = [keep.tile([P, X_WINDOW], U32, name=f"x_codes{a}", align_bytes=64) for a in range(PASSES)]
         x_scales = keep.tile([P, X_WINDOW], U8, name="x_scales", align_bytes=64)
         picked_scales = keep.tile([P, S], U8, name="picked_scales", align_bytes=64)
@@ -69,25 +65,23 @@ def tile_picked_tome_lin_relu2_sub_e_kernel(tc, xT, w, b, gate, offs, out):
                 t0 += n
             if a == 0:
                 nc.sync.dma_start(offsets[:], offs)
-        for a in range(PASSES):
-            for i, g in enumerate(W_LOADS[a]):
-                src = w[g[0] : g[-1] + 1, a * PASS_K : (a + 1) * PASS_K, :].rearrange("d (p j) m -> p d j m", j=PACK)
-                nc.sync.dma_start(out=w_in[a][i][:], in_=src)
+        for i, (a, lo, hi) in enumerate(W_LOADS):
+            src = w[lo:hi, a * PASS_K : (a + 1) * PASS_K, :].rearrange("d (p j) m -> p d j m", j=PACK)
+            nc.sync.dma_start(out=w_raw[i][:], in_=src)
         nc.sync.dma_start(out=gates[:], in_=gate)
 
         nc.gpsimd.memset(x_scales[:], 0)
         for a in range(PASSES):
             nc.gpsimd.memset(x_codes[a][:, T:X_WINDOW], 0)
 
-        def interleave(copy, dst, src):
-            copy(out=dst.rearrange("p (c i) j -> p c j i", i=RUN), in_=src.rearrange("p j (c i) -> p c j i", i=RUN))
-
         def shared_interleave(dst, src, on_vector):
-            mid = dst.shape[1] - on_vector
-            if mid > 0:
-                interleave(nc.scalar.copy, dst[:, 0:mid, :], src[:, :, 0:mid])
-            if on_vector > 0:
-                interleave(nc.vector.tensor_copy, dst[:, mid:, :], src[:, :, mid:])
+            mid = dst.shape[2] - on_vector
+            for copy, cols, run in ((nc.scalar.copy, slice(0, mid), RUN), (nc.vector.tensor_copy, slice(mid, dst.shape[2]), RUN)):
+                if cols.stop > cols.start:
+                    copy(
+                        out=dst[:, :, cols, :].rearrange("p d (c i) j -> p d c j i", i=run),
+                        in_=src[:, :, :, cols].rearrange("p d j (c i) -> p d c j i", i=run),
+                    )
 
         def x_half(a, c):
             if len(X_SPLIT[a]) == 2:
@@ -102,15 +96,16 @@ def tile_picked_tome_lin_relu2_sub_e_kernel(tc, xT, w, b, gate, offs, out):
                 in_=x_bf[a][c][:].rearrange("p t j -> p (t j)"),
             )
 
-        def weights(a, i):
-            g = W_GROUPS[a][i]
-            for n, d in enumerate(g):
-                shared_interleave(w_bf[a][i][:, n, :, :], w_raw[a][d], W_VECTOR[a][d])
-            cols = slice(g[0] * N, (g[-1] + 1) * N)
+        def weights(i):
+            a, lo, hi = W_LOADS[i]
+            tag = f"w_slot{i - 1}" if i == len(W_LOADS) - 1 else f"w_bf{i}"
+            w_bf = keep.tile([P, hi - lo, N, PACK], BF16, name=f"w_bf{i}", tag=tag, align_bytes=64)
+            shared_interleave(w_bf[:], w_raw[i][:], W_VECTOR[i])
+            cols = slice(lo * N, hi * N)
             nc.vector.quantize_mx(
                 out=w_codes[a][:, cols].bitcast(FP8X4),
                 scales=w_scales[a][:, cols],
-                in_=w_bf[a][i][:].rearrange("p d m j -> p (d m j)"),
+                in_=w_bf[:].rearrange("p d m j -> p (d m j)"),
             )
 
         picked = {}
@@ -136,19 +131,18 @@ def tile_picked_tome_lin_relu2_sub_e_kernel(tc, xT, w, b, gate, offs, out):
 
         for a in range(PASSES):
             for c in range(2):
-                shared_interleave(x_bf[a][c][:], x_half(a, c), X_VECTOR[a][c])
+                shared_interleave(x_bf[a][c][:].unsqueeze(1), x_half(a, c).unsqueeze(1), X_VECTOR[a][c])
             for c in range(2):
                 quantize_x(a, c)
             if a < LAST:
-                gather_codes(a, 0, S, f"head{a}")
+                gather_codes(a, 0, S, f"picked{a}")
         nc.vector.tensor_copy(picked_scales[:], x_scales[:].indirect(offsets[:]))
-        for a in range(PASSES):
-            for i, g in enumerate(W_GROUPS[a]):
-                weights(a, i)
-                if a in (1, 2) and i == 0:
-                    gather_codes(LAST, (a - 1) * HALF, a * HALF, f"w_in{a}_0")
-                for d in g:
-                    multiply(a, d)
+        for i, (a, lo, hi) in enumerate(W_LOADS):
+            weights(i)
+            if i < 2:
+                gather_codes(LAST, i * HALF, (i + 1) * HALF, f"w_slot{i}")
+            for d in range(lo, hi):
+                multiply(a, d)
 
         halves = [slice(0, VH), slice(VH, V)]
         for h in (0, 1):

@@ -23,12 +23,12 @@ HALF = T // 2
 X_WINDOW = 1408
 OUT_WINDOW = 2048
 VH = V // 2
-RUN = 2
+RUN = 4
 
-X_VECTOR = ((256, 256), (192, 192), (192, 192), (0, 128))
+X_VECTOR = ((288, 288), (224, 224), (160, 160), (0, 128))
 X_SPLIT = ((1024,), (1024,), (1024,), (512, 512))
 W_LOADS = ((0, 0, 4), (1, 0, 4), (2, 0, 4), (3, 0, 2), (3, 2, 3), (3, 3, 4))
-W_VECTOR = (0, 0, 32, 0, 0, 64)
+W_VECTOR = (32, 0, 32, 0, 64, 64)
 
 
 def tile_picked_tome_lin_relu2_sub_e_kernel(tc, xT, w, b, gate, offs, out):
@@ -68,7 +68,8 @@ def tile_picked_tome_lin_relu2_sub_e_kernel(tc, xT, w, b, gate, offs, out):
         for i, (a, lo, hi) in enumerate(W_LOADS):
             src = w[lo:hi, a * PASS_K : (a + 1) * PASS_K, :].rearrange("d (p j) m -> p d j m", j=PACK)
             nc.sync.dma_start(out=w_raw[i][:], in_=src)
-        nc.sync.dma_start(out=gates[:], in_=gate)
+        for c in range(2):
+            nc.sync.dma_start(out=gates[:, c * HALF : (c + 1) * HALF], in_=gate[:, c * HALF : (c + 1) * HALF])
 
         nc.gpsimd.memset(x_scales[:], 0)
         for a in range(PASSES):
@@ -98,7 +99,7 @@ def tile_picked_tome_lin_relu2_sub_e_kernel(tc, xT, w, b, gate, offs, out):
 
         def weights(i):
             a, lo, hi = W_LOADS[i]
-            tag = f"w_slot{i - 1}" if i == len(W_LOADS) - 1 else f"w_bf{i}"
+            tag = f"w_slot{i - 1}" if i == 4 else f"w_bf{i}"
             w_bf = keep.tile([P, hi - lo, N, PACK], BF16, name=f"w_bf{i}", tag=tag, align_bytes=64)
             shared_interleave(w_bf[:], w_raw[i][:], W_VECTOR[i])
             cols = slice(lo * N, hi * N)
@@ -140,13 +141,13 @@ def tile_picked_tome_lin_relu2_sub_e_kernel(tc, xT, w, b, gate, offs, out):
         for i, (a, lo, hi) in enumerate(W_LOADS):
             weights(i)
             if i < 2:
-                gather_codes(LAST, i * HALF, (i + 1) * HALF, f"w_slot{i}")
+                gather_codes(LAST, i * HALF, (i + 1) * HALF, f"w_bf{i}")
             for d in range(lo, hi):
                 multiply(a, d)
 
         halves = [slice(0, VH), slice(VH, V)]
-        for h in (0, 1):
-            nc.scalar.activation(out=r[:, halves[h]], in_=acc[h][:], func=ACT.Relu, bias=bias[:, 0:1])
+        nc.scalar.activation(out=r[:, halves[0]], in_=acc[0][:], func=ACT.Relu, bias=bias[:, 0:1])
+        nc.vector.tensor_scalar(out=r[:, halves[1]], in0=acc[1][:], scalar1=bias[:, 0:1], scalar2=0.0, op0=ALU.add, op1=ALU.max)
         for h in (1, 0):
             nc.vector.scalar_tensor_tensor(
                 out=ug[:, halves[h]], in0=acc[h][:], scalar=bias[:, 0:1], in1=gates[:, halves[h]], op0=ALU.add, op1=ALU.mult

@@ -25,9 +25,10 @@ OUT_WINDOW = 2048
 VH = V // 2
 RUN = 4
 
-X_VECTOR = ((288, 288), (224, 224), (160, 160), (0, 128))
+X_VECTOR = ((256, 256), (208, 208), (160, 160), (0, 128))
 X_SPLIT = ((1024,), (1024,), (1024,), (512, 512))
-W_LOADS = ((0, 0, 4), (1, 0, 4), (2, 0, 4), (3, 0, 2), (3, 2, 3), (3, 3, 4))
+W_LOADS = ((0, 0, 4), (1, 0, 4), (2, 0, 4), (3, 0, 3), (3, 3, 4))
+W_GROUPS = ((0, 0, 4), (1, 0, 4), (2, 0, 4), (3, 0, 2), (3, 2, 3), (3, 3, 4))
 W_VECTOR = (32, 0, 32, 0, 64, 64)
 
 
@@ -42,7 +43,7 @@ def tile_picked_tome_lin_relu2_sub_e_kernel(tc, xT, w, b, gate, offs, out):
         gates = keep.tile([P, S], F32, name="gates")
         x_raw = [[keep.tile([P, PACK, n], F32, name=f"x_raw{a}_{i}") for i, n in enumerate(X_SPLIT[a])] for a in range(PASSES)]
         w_raw = [
-            keep.tile([P, hi - lo, PACK, N], F32, name=f"w_raw{i}", tag=f"w_slot{i}", align_bytes=64) for i, (a, lo, hi) in enumerate(W_LOADS)
+            keep.tile([P, hi - lo, PACK, N], F32, name=f"w_raw{i}") for i, (a, lo, hi) in enumerate(W_LOADS)
         ]
         x_bf = [[keep.tile([P, HALF, PACK], BF16, name=f"x_bf{a}_{c}", align_bytes=64) for c in range(2)] for a in range(PASSES)]
         x_codes = [keep.tile([P, X_WINDOW], U32, name=f"x_codes{a}", align_bytes=64) for a in range(PASSES)]
@@ -56,7 +57,6 @@ def tile_picked_tome_lin_relu2_sub_e_kernel(tc, xT, w, b, gate, offs, out):
         result = keep.tile([P, OUT_WINDOW], F32, name="result")
         acc = [psum.tile([P, VH], F32, name=f"acc{h}") for h in range(2)]
 
-        nc.scalar.dma_start(out=bias[:], in_=b)
         for a in range(PASSES):
             t0 = 0
             for i, n in enumerate(X_SPLIT[a]):
@@ -68,6 +68,7 @@ def tile_picked_tome_lin_relu2_sub_e_kernel(tc, xT, w, b, gate, offs, out):
         for i, (a, lo, hi) in enumerate(W_LOADS):
             src = w[lo:hi, a * PASS_K : (a + 1) * PASS_K, :].rearrange("d (p j) m -> p d j m", j=PACK)
             nc.sync.dma_start(out=w_raw[i][:], in_=src)
+        nc.sync.dma_start(out=bias[:], in_=b)
         for c in range(2):
             nc.sync.dma_start(out=gates[:, c * HALF : (c + 1) * HALF], in_=gate[:, c * HALF : (c + 1) * HALF])
 
@@ -98,10 +99,10 @@ def tile_picked_tome_lin_relu2_sub_e_kernel(tc, xT, w, b, gate, offs, out):
             )
 
         def weights(i):
-            a, lo, hi = W_LOADS[i]
-            tag = f"w_slot{i - 1}" if i == 4 else f"w_bf{i}"
-            w_bf = keep.tile([P, hi - lo, N, PACK], BF16, name=f"w_bf{i}", tag=tag, align_bytes=64)
-            shared_interleave(w_bf[:], w_raw[i][:], W_VECTOR[i])
+            a, lo, hi = W_GROUPS[i]
+            n, first = [(n, load[1]) for n, load in enumerate(W_LOADS) if load[0] == a and load[1] <= lo < load[2]][0]
+            w_bf = keep.tile([P, hi - lo, N, PACK], BF16, name=f"w_bf{i}", tag=f"w_bf{i}", align_bytes=64)
+            shared_interleave(w_bf[:], w_raw[n][:, lo - first : hi - first, :, :], W_VECTOR[i])
             cols = slice(lo * N, hi * N)
             nc.vector.quantize_mx(
                 out=w_codes[a][:, cols].bitcast(FP8X4),
@@ -138,7 +139,7 @@ def tile_picked_tome_lin_relu2_sub_e_kernel(tc, xT, w, b, gate, offs, out):
             if a < LAST:
                 gather_codes(a, 0, S, f"picked{a}")
         nc.vector.tensor_copy(picked_scales[:], x_scales[:].indirect(offsets[:]))
-        for i, (a, lo, hi) in enumerate(W_LOADS):
+        for i, (a, lo, hi) in enumerate(W_GROUPS):
             weights(i)
             if i < 2:
                 gather_codes(LAST, i * HALF, (i + 1) * HALF, f"w_bf{i}")

@@ -25,11 +25,12 @@ OUT_WINDOW = 2048
 VH = V // 2
 RUN = 4
 
-X_VECTOR = ((256, 256), (208, 208), (160, 160), (0, 128))
-X_SPLIT = ((1024,), (1024,), (1024,), (512, 512))
-W_LOADS = ((0, 0, 4), (1, 0, 4), (2, 0, 4), (3, 0, 3), (3, 3, 4))
-W_GROUPS = ((0, 0, 4), (1, 0, 4), (2, 0, 4), (3, 0, 2), (3, 2, 3), (3, 3, 4))
-W_VECTOR = (32, 0, 32, 0, 64, 64)
+X_PIECES = ((0, 256), (256, 768), (768, 1024))
+X_VECTOR_FIRST, X_VECTOR_STEP = 512, 56
+DEFERRED = 256
+W_LOADS = ((0, 0, 2), (0, 2, 4), (1, 0, 2), (1, 2, 4), (2, 0, 2), (2, 2, 4), (3, 0, 1), (3, 1, 2), (3, 2, 3), (3, 3, 4))
+W_VECTOR = {3: 64, 9: 64}
+GATHER_AFTER = {0: 0, 2: 1, 4: 2, 5: 3}
 
 
 def tile_picked_tome_lin_relu2_sub_e_kernel(tc, xT, w, b, gate, offs, out):
@@ -41,12 +42,12 @@ def tile_picked_tome_lin_relu2_sub_e_kernel(tc, xT, w, b, gate, offs, out):
         offsets = keep.tile([P, S // 16], U16, name="offsets")
         bias = keep.tile([P, 1], F32, name="bias")
         gates = keep.tile([P, S], F32, name="gates")
-        x_raw = [[keep.tile([P, PACK, n], F32, name=f"x_raw{a}_{i}") for i, n in enumerate(X_SPLIT[a])] for a in range(PASSES)]
+        x_raw = [keep.tile([P, PACK, T], F32, name=f"x_raw{a}", tag=f"x_raw{a}", align_bytes=64) for a in range(PASSES)]
         w_raw = [
-            keep.tile([P, hi - lo, PACK, N], F32, name=f"w_raw{i}") for i, (a, lo, hi) in enumerate(W_LOADS)
+            keep.tile([P, hi - lo, PACK, N], F32, name=f"w_raw{i}", tag=f"w_raw{i}", align_bytes=64)
+            for i, (a, lo, hi) in enumerate(W_LOADS)
         ]
-        x_bf = [[keep.tile([P, HALF, PACK], BF16, name=f"x_bf{a}_{c}", align_bytes=64) for c in range(2)] for a in range(PASSES)]
-        x_codes = [keep.tile([P, X_WINDOW], U32, name=f"x_codes{a}", align_bytes=64) for a in range(PASSES)]
+        x_codes = [keep.tile([P, T], U32, name=f"x_codes{a}", align_bytes=64) for a in range(PASSES)]
         x_scales = keep.tile([P, X_WINDOW], U8, name="x_scales", align_bytes=64)
         picked_scales = keep.tile([P, S], U8, name="picked_scales", align_bytes=64)
         w_codes = [keep.tile([P, D * N], U32, name=f"w_codes{a}", align_bytes=64) for a in range(PASSES)]
@@ -58,11 +59,8 @@ def tile_picked_tome_lin_relu2_sub_e_kernel(tc, xT, w, b, gate, offs, out):
         acc = [psum.tile([P, VH], F32, name=f"acc{h}") for h in range(2)]
 
         for a in range(PASSES):
-            t0 = 0
-            for i, n in enumerate(X_SPLIT[a]):
-                src = xT[a * PASS_K : (a + 1) * PASS_K, t0 : t0 + n]
-                nc.sync.dma_start(out=x_raw[a][i][:], in_=src.rearrange("(p j) t -> p j t", j=PACK))
-                t0 += n
+            src = xT[a * PASS_K : (a + 1) * PASS_K, :]
+            nc.sync.dma_start(out=x_raw[a][:], in_=src.rearrange("(p j) t -> p j t", j=PACK))
             if a == 0:
                 nc.sync.dma_start(offsets[:], offs)
         for i, (a, lo, hi) in enumerate(W_LOADS):
@@ -73,42 +71,19 @@ def tile_picked_tome_lin_relu2_sub_e_kernel(tc, xT, w, b, gate, offs, out):
             nc.sync.dma_start(out=gates[:, c * HALF : (c + 1) * HALF], in_=gate[:, c * HALF : (c + 1) * HALF])
 
         nc.gpsimd.memset(x_scales[:], 0)
-        for a in range(PASSES):
-            nc.gpsimd.memset(x_codes[a][:, T:X_WINDOW], 0)
+
+        def interleave(copy, dst, src):
+            copy(
+                out=dst.rearrange("p d (c i) j -> p d c j i", i=RUN),
+                in_=src.rearrange("p d j (c i) -> p d c j i", i=RUN),
+            )
 
         def shared_interleave(dst, src, on_vector):
-            mid = dst.shape[2] - on_vector
-            for copy, cols, run in ((nc.scalar.copy, slice(0, mid), RUN), (nc.vector.tensor_copy, slice(mid, dst.shape[2]), RUN)):
-                if cols.stop > cols.start:
-                    copy(
-                        out=dst[:, :, cols, :].rearrange("p d (c i) j -> p d c j i", i=run),
-                        in_=src[:, :, :, cols].rearrange("p d j (c i) -> p d c j i", i=run),
-                    )
-
-        def x_half(a, c):
-            if len(X_SPLIT[a]) == 2:
-                return x_raw[a][c][:]
-            return x_raw[a][0][:, :, c * HALF : (c + 1) * HALF]
-
-        def quantize_x(a, c):
-            cols = slice(c * HALF, (c + 1) * HALF)
-            nc.vector.quantize_mx(
-                out=x_codes[a][:, cols].bitcast(FP8X4),
-                scales=x_scales[4 * a : P, cols],
-                in_=x_bf[a][c][:].rearrange("p t j -> p (t j)"),
-            )
-
-        def weights(i):
-            a, lo, hi = W_GROUPS[i]
-            n, first = [(n, load[1]) for n, load in enumerate(W_LOADS) if load[0] == a and load[1] <= lo < load[2]][0]
-            w_bf = keep.tile([P, hi - lo, N, PACK], BF16, name=f"w_bf{i}", tag=f"w_bf{i}", align_bytes=64)
-            shared_interleave(w_bf[:], w_raw[n][:, lo - first : hi - first, :, :], W_VECTOR[i])
-            cols = slice(lo * N, hi * N)
-            nc.vector.quantize_mx(
-                out=w_codes[a][:, cols].bitcast(FP8X4),
-                scales=w_scales[a][:, cols],
-                in_=w_bf[:].rearrange("p d m j -> p (d m j)"),
-            )
+            width = dst.shape[2]
+            if on_vector > 0:
+                interleave(nc.vector.tensor_copy, dst[:, :, 0:on_vector, :], src[:, :, :, 0:on_vector])
+            if on_vector < width:
+                interleave(nc.scalar.copy, dst[:, :, on_vector:width, :], src[:, :, :, on_vector:width])
 
         picked = {}
 
@@ -118,33 +93,47 @@ def tile_picked_tome_lin_relu2_sub_e_kernel(tc, xT, w, b, gate, offs, out):
             for s in range(lo, hi, VH):
                 picked[a, s] = dst[:, s - lo : s - lo + VH]
 
-        def multiply(a, d):
-            for h in range(2):
-                s = d * V + h * VH
-                nc.tensor.matmul_mx(
-                    out=acc[h][:],
-                    lhsT=w_codes[a][:, d * N : (d + 1) * N].bitcast(FP8X4),
-                    lhsT_scale=w_scales[a][:, d * N : (d + 1) * N],
-                    rhs=picked[a, s].bitcast(FP8X4),
-                    rhs_scale=picked_scales[4 * a : P, s : s + VH],
-                    start=(a == 0 and d == 0),
-                    stop=(a == LAST and d == D - 1),
-                )
-
         for a in range(PASSES):
-            for c in range(2):
-                shared_interleave(x_bf[a][c][:].unsqueeze(1), x_half(a, c).unsqueeze(1), X_VECTOR[a][c])
-            for c in range(2):
-                quantize_x(a, c)
+            for lo, hi in X_PIECES:
+                x_bf = keep.tile([P, hi - lo, PACK], BF16, name=f"x_bf{a}_{lo}", align_bytes=64)
+                on_vector = X_VECTOR_FIRST - X_VECTOR_STEP * a if hi - lo == HALF else 0
+                shared_interleave(x_bf[:].unsqueeze(1), x_raw[a][:, :, lo:hi].unsqueeze(1), on_vector)
+                nc.vector.quantize_mx(
+                    out=x_codes[a][:, lo:hi].bitcast(FP8X4),
+                    scales=x_scales[4 * a : P, lo:hi],
+                    in_=x_bf[:].rearrange("p t j -> p (t j)"),
+                )
+            if a > 0:
+                gather_codes(a - 1, S - DEFERRED, S, f"x_raw{a}")
             if a < LAST:
-                gather_codes(a, 0, S, f"picked{a}")
+                gather_codes(a, 0, S - DEFERRED, f"picked{a}")
         nc.vector.tensor_copy(picked_scales[:], x_scales[:].indirect(offsets[:]))
-        for i, (a, lo, hi) in enumerate(W_GROUPS):
-            weights(i)
-            if i < 2:
-                gather_codes(LAST, i * HALF, (i + 1) * HALF, f"w_bf{i}")
+
+        for i, (a, lo, hi) in enumerate(W_LOADS):
+            held_by = f"w_raw{i - 2}" if i in W_VECTOR else f"w_bf{i}"
+            w_bf = keep.tile([P, hi - lo, N, PACK], BF16, name=f"w_bf{i}", tag=held_by, align_bytes=64)
+            shared_interleave(w_bf[:], w_raw[i][:], W_VECTOR.get(i, 0))
+            cols = slice(lo * N, hi * N)
+            nc.vector.quantize_mx(
+                out=w_codes[a][:, cols].bitcast(FP8X4),
+                scales=w_scales[a][:, cols],
+                in_=w_bf[:].rearrange("p d m j -> p (d m j)"),
+            )
+            if i in GATHER_AFTER:
+                c = GATHER_AFTER[i]
+                gather_codes(LAST, c * V, (c + 1) * V, f"w_raw{i}")
             for d in range(lo, hi):
-                multiply(a, d)
+                for h in range(2):
+                    s = d * V + h * VH
+                    nc.tensor.matmul_mx(
+                        out=acc[h][:],
+                        lhsT=w_codes[a][:, d * N : (d + 1) * N].bitcast(FP8X4),
+                        lhsT_scale=w_scales[a][:, d * N : (d + 1) * N],
+                        rhs=picked[a, s].bitcast(FP8X4),
+                        rhs_scale=picked_scales[4 * a : P, s : s + VH],
+                        start=(a == 0 and d == 0),
+                        stop=(a == LAST and d == D - 1),
+                    )
 
         halves = [slice(0, VH), slice(VH, V)]
         nc.scalar.activation(out=r[:, halves[0]], in_=acc[0][:], func=ACT.Relu, bias=bias[:, 0:1])

@@ -29,7 +29,7 @@ X_PIECES = ((0, 256), (256, 768), (768, 1024))
 X_VECTOR_FIRST, X_VECTOR_STEP = 512, 56
 DEFERRED = 256
 W_LOADS = ((0, 0, 2), (0, 2, 4), (1, 0, 2), (1, 2, 4), (2, 0, 2), (2, 2, 4), (3, 0, 1), (3, 1, 2), (3, 2, 3), (3, 3, 4))
-W_VECTOR = {3: 64, 9: 64}
+W_VECTOR = {9: 64}
 GATHER_AFTER = {0: 0, 2: 1, 4: 2, 5: 3}
 
 
@@ -95,7 +95,7 @@ def tile_picked_tome_lin_relu2_sub_e_kernel(tc, xT, w, b, gate, offs, out):
 
         for a in range(PASSES):
             for lo, hi in X_PIECES:
-                x_bf = keep.tile([P, hi - lo, PACK], BF16, name=f"x_bf{a}_{lo}", align_bytes=64)
+                x_bf = keep.tile([P, hi - lo, PACK], BF16, name=f"x_bf{a}_{lo}", tag=f"x_bf{a}_{lo}", align_bytes=64)
                 on_vector = X_VECTOR_FIRST - X_VECTOR_STEP * a if hi - lo == HALF else 0
                 shared_interleave(x_bf[:].unsqueeze(1), x_raw[a][:, :, lo:hi].unsqueeze(1), on_vector)
                 nc.vector.quantize_mx(
@@ -111,8 +111,15 @@ def tile_picked_tome_lin_relu2_sub_e_kernel(tc, xT, w, b, gate, offs, out):
 
         for i, (a, lo, hi) in enumerate(W_LOADS):
             held_by = f"w_raw{i - 2}" if i in W_VECTOR else f"w_bf{i}"
+            if i == 0:
+                held_by = f"x_bf{LAST}_{X_PIECES[-1][0]}"
             w_bf = keep.tile([P, hi - lo, N, PACK], BF16, name=f"w_bf{i}", tag=held_by, align_bytes=64)
-            shared_interleave(w_bf[:], w_raw[i][:], W_VECTOR.get(i, 0))
+            if i == 0:
+                nc.gpsimd.tensor_scalar(
+                    out=w_bf[:], in0=w_raw[i][:].rearrange("p d j m -> p d m j"), scalar1=1.0, scalar2=0.0, op0=ALU.mult, op1=ALU.add
+                )
+            else:
+                shared_interleave(w_bf[:], w_raw[i][:], W_VECTOR.get(i, 0))
             cols = slice(lo * N, hi * N)
             nc.vector.quantize_mx(
                 out=w_codes[a][:, cols].bitcast(FP8X4),

@@ -26,32 +26,37 @@ VH = V // 2
 RUN = 4
 
 X_PIECES = ((0, 256), (256, 768), (768, 1024))
-X_VECTOR_FIRST, X_VECTOR_STEP = 512, 56
+X_VECTOR_FIRST, X_VECTOR_LATER = 512, 320
+X_GPSIMD = 128
 DEFERRED = 256
-W_LOADS = ((0, 0, 2), (0, 2, 4), (1, 0, 2), (1, 2, 4), (2, 0, 2), (2, 2, 4), (3, 0, 1), (3, 1, 2), (3, 2, 3), (3, 3, 4))
-W_VECTOR = {9: 64}
-GATHER_AFTER = {0: 0, 2: 1, 4: 2, 5: 3}
+W_LOADS = ((0, 0, 2), (0, 2, 4), (1, 0, 2), (1, 2, 4)) + tuple((a, d, d + 1) for a in (2, 3) for d in range(D))
+W_GPSIMD = (1, 2)
+W_VECTOR = {11: 64}
+GATHER_AFTER = {1: 0, 3: 1, 5: 2, 7: 3}
+RAW_AT = {1: 0, 2: 4096, 9: 8192}
 
 
 def tile_picked_tome_lin_relu2_sub_e_kernel(tc, xT, w, b, gate, offs, out):
     nc = tc.nc
     with ExitStack() as ctx:
         keep = ctx.enter_context(tc.tile_pool(name="keep", bufs=1))
+        reused = ctx.enter_context(tc.tile_pool(name="reused", bufs=1))
         psum = ctx.enter_context(tc.psum_pool(name="psum", bufs=1))
 
         offsets = keep.tile([P, S // 16], U16, name="offsets")
         bias = keep.tile([P, 1], F32, name="bias")
         gates = keep.tile([P, S], F32, name="gates")
         x_raw = [keep.tile([P, PACK, T], F32, name=f"x_raw{a}", tag=f"x_raw{a}", align_bytes=64) for a in range(PASSES)]
-        w_raw = [
-            keep.tile([P, hi - lo, PACK, N], F32, name=f"w_raw{i}", tag=f"w_raw{i}", align_bytes=64)
-            for i, (a, lo, hi) in enumerate(W_LOADS)
-        ]
+        w_raw = []
+        for i, (a, lo, hi) in enumerate(W_LOADS):
+            if i in RAW_AT:
+                w_raw.append(reused.tile([P, hi - lo, PACK, N], F32, name=f"w_raw{i}", align_bytes=64, offset=RAW_AT[i]))
+            else:
+                w_raw.append(keep.tile([P, hi - lo, PACK, N], F32, name=f"w_raw{i}", align_bytes=64))
         x_codes = [keep.tile([P, T], U32, name=f"x_codes{a}", align_bytes=64) for a in range(PASSES)]
         x_scales = keep.tile([P, X_WINDOW], U8, name="x_scales", align_bytes=64)
         picked_scales = keep.tile([P, S], U8, name="picked_scales", align_bytes=64)
         w_codes = [keep.tile([P, D * N], U32, name=f"w_codes{a}", align_bytes=64) for a in range(PASSES)]
-        w_scales = [keep.tile([P, D * N], U8, name=f"w_scales{a}", align_bytes=64) for a in range(PASSES)]
         r = keep.tile([P, V], F32, name="r")
         ug = keep.tile([P, V], F32, name="ug")
         y = keep.tile([P, D - 1, V], F32, name="y")
@@ -87,48 +92,64 @@ def tile_picked_tome_lin_relu2_sub_e_kernel(tc, xT, w, b, gate, offs, out):
 
         picked = {}
 
-        def gather_codes(a, lo, hi, tag):
-            dst = keep.tile([P, hi - lo], U32, name=f"picked{a}_{lo}", tag=tag, align_bytes=64)
-            nc.vector.tensor_copy(dst[:], x_codes[a][:].indirect(offsets[:, lo // 16 : hi // 16]))
+        def picked_tile(a, lo, hi, tag):
+            return keep.tile([P, hi - lo], U32, name=f"picked{a}_{lo}", tag=tag, align_bytes=64)[:]
+
+        def gather_codes(a, lo, hi, dst):
+            nc.vector.tensor_copy(dst, x_codes[a][:].indirect(offsets[:, lo // 16 : hi // 16]))
             for s in range(lo, hi, VH):
                 picked[a, s] = dst[:, s - lo : s - lo + VH]
 
         for a in range(PASSES):
             for lo, hi in X_PIECES:
-                x_bf = keep.tile([P, hi - lo, PACK], BF16, name=f"x_bf{a}_{lo}", tag=f"x_bf{a}_{lo}", align_bytes=64)
-                on_vector = X_VECTOR_FIRST - X_VECTOR_STEP * a if hi - lo == HALF else 0
-                shared_interleave(x_bf[:].unsqueeze(1), x_raw[a][:, :, lo:hi].unsqueeze(1), on_vector)
+                tag = "ring" if hi == T else f"x_bf{a}_{lo}"
+                x_bf = keep.tile([P, hi - lo, PACK], BF16, name=f"x_bf{a}_{lo}", tag=tag, align_bytes=64)
+                if hi == T and a > 0:
+                    mid = hi - lo - X_GPSIMD
+                    interleave(nc.scalar.copy, x_bf[:, 0:mid, :].unsqueeze(1), x_raw[a][:, :, lo : lo + mid].unsqueeze(1))
+                    nc.gpsimd.tensor_copy(out=x_bf[:, mid : hi - lo, :], in_=x_raw[a][:, :, lo + mid : hi].rearrange("p j t -> p t j"))
+                else:
+                    on_vector = (X_VECTOR_LATER if a > 0 else X_VECTOR_FIRST) if hi - lo == HALF else 0
+                    shared_interleave(x_bf[:].unsqueeze(1), x_raw[a][:, :, lo:hi].unsqueeze(1), on_vector)
                 nc.vector.quantize_mx(
                     out=x_codes[a][:, lo:hi].bitcast(FP8X4),
                     scales=x_scales[4 * a : P, lo:hi],
                     in_=x_bf[:].rearrange("p t j -> p (t j)"),
                 )
             if a > 0:
-                gather_codes(a - 1, S - DEFERRED, S, f"x_raw{a}")
+                gather_codes(a - 1, S - DEFERRED, S, picked_tile(a - 1, S - DEFERRED, S, f"x_raw{a}"))
             if a < LAST:
-                gather_codes(a, 0, S - DEFERRED, f"picked{a}")
+                gather_codes(a, 0, S - DEFERRED, picked_tile(a, 0, S - DEFERRED, f"picked{a}"))
         nc.vector.tensor_copy(picked_scales[:], x_scales[:].indirect(offsets[:]))
 
+        w_scales = {0: reused.tile([P, D * N], U8, name="w_scales0", align_bytes=64, offset=0)[:]}
+        picked_last = reused.tile([P, S], U32, name="picked_last", align_bytes=64, offset=1024)
+        later_scales = reused.tile([P, LAST * D * N], U8, name="later_scales", align_bytes=64, offset=5120)
+        for c in range(1, PASSES):
+            w_scales[c] = later_scales[:, (c - 1) * D * N : c * D * N]
+        gpsimd_bf = keep.tile([P, 4, N, PACK], BF16, name="gpsimd_bf", tag="ring", align_bytes=64)
         for i, (a, lo, hi) in enumerate(W_LOADS):
-            held_by = f"w_raw{i - 2}" if i in W_VECTOR else f"w_bf{i}"
-            if i == 0:
-                held_by = f"x_bf{LAST}_{X_PIECES[-1][0]}"
-            w_bf = keep.tile([P, hi - lo, N, PACK], BF16, name=f"w_bf{i}", tag=held_by, align_bytes=64)
-            if i == 0:
+            if i in W_GPSIMD:
+                k = 2 * W_GPSIMD.index(i)
+                w_bf = gpsimd_bf[:, k : k + 2, :, :]
                 nc.gpsimd.tensor_scalar(
-                    out=w_bf[:], in0=w_raw[i][:].rearrange("p d j m -> p d m j"), scalar1=1.0, scalar2=0.0, op0=ALU.mult, op1=ALU.add
+                    out=w_bf, in0=w_raw[i][:].rearrange("p d j m -> p d m j"), scalar1=1.0, scalar2=0.0, op0=ALU.mult, op1=ALU.add
                 )
             else:
-                shared_interleave(w_bf[:], w_raw[i][:], W_VECTOR.get(i, 0))
+                if i in W_VECTOR:
+                    w_bf = reused.tile([P, hi - lo, N, PACK], BF16, name=f"w_bf{i}", align_bytes=64, offset=7680)[:]
+                else:
+                    w_bf = keep.tile([P, hi - lo, N, PACK], BF16, name=f"w_bf{i}", align_bytes=64)[:]
+                shared_interleave(w_bf, w_raw[i][:], W_VECTOR.get(i, 0))
             cols = slice(lo * N, hi * N)
             nc.vector.quantize_mx(
                 out=w_codes[a][:, cols].bitcast(FP8X4),
                 scales=w_scales[a][:, cols],
-                in_=w_bf[:].rearrange("p d m j -> p (d m j)"),
+                in_=w_bf.rearrange("p d m j -> p (d m j)"),
             )
             if i in GATHER_AFTER:
                 c = GATHER_AFTER[i]
-                gather_codes(LAST, c * V, (c + 1) * V, f"w_raw{i}")
+                gather_codes(LAST, c * V, (c + 1) * V, picked_last[:, c * V : (c + 1) * V])
             for d in range(lo, hi):
                 for h in range(2):
                     s = d * V + h * VH

@@ -26,14 +26,13 @@ VH = V // 2
 RUN = 4
 
 X_PIECES = ((0, 256), (256, 768), (768, 1024))
-X_VECTOR_FIRST, X_VECTOR_LATER = 512, 320
-X_GPSIMD = 128
+X_VECTOR_FIRST, X_VECTOR_STEP = 512, 56
 DEFERRED = 256
-W_LOADS = ((0, 0, 2), (0, 2, 4), (1, 0, 2), (1, 2, 4)) + tuple((a, d, d + 1) for a in (2, 3) for d in range(D))
-W_GPSIMD = (1, 2)
+W_LOADS = ((0, 0, 3), (0, 3, 4), (1, 0, 2), (1, 2, 4)) + tuple((a, d, d + 1) for a in (2, 3) for d in range(D))
 W_VECTOR = {11: 64}
-GATHER_AFTER = {1: 0, 3: 1, 5: 2, 7: 3}
-RAW_AT = {1: 0, 2: 4096, 9: 8192}
+GATHER_AFTER = {3: (0, 1), 5: (1, 2), 8: (2, 4)}
+RAW_AT = {3: 0, 0: 4096, 5: 10240, 8: 12288, 9: 14336}
+PICKED_AT = {3: 3584, 5: 9728, 8: 12288}
 
 
 def tile_picked_tome_lin_relu2_sub_e_kernel(tc, xT, w, b, gate, offs, out):
@@ -102,15 +101,10 @@ def tile_picked_tome_lin_relu2_sub_e_kernel(tc, xT, w, b, gate, offs, out):
 
         for a in range(PASSES):
             for lo, hi in X_PIECES:
-                tag = "ring" if hi == T else f"x_bf{a}_{lo}"
+                tag = "ring" if hi == T and a == LAST else f"x_bf{a}_{lo}"
                 x_bf = keep.tile([P, hi - lo, PACK], BF16, name=f"x_bf{a}_{lo}", tag=tag, align_bytes=64)
-                if hi == T and a > 0:
-                    mid = hi - lo - X_GPSIMD
-                    interleave(nc.scalar.copy, x_bf[:, 0:mid, :].unsqueeze(1), x_raw[a][:, :, lo : lo + mid].unsqueeze(1))
-                    nc.gpsimd.tensor_copy(out=x_bf[:, mid : hi - lo, :], in_=x_raw[a][:, :, lo + mid : hi].rearrange("p j t -> p t j"))
-                else:
-                    on_vector = (X_VECTOR_LATER if a > 0 else X_VECTOR_FIRST) if hi - lo == HALF else 0
-                    shared_interleave(x_bf[:].unsqueeze(1), x_raw[a][:, :, lo:hi].unsqueeze(1), on_vector)
+                on_vector = X_VECTOR_FIRST - X_VECTOR_STEP * a if hi - lo == HALF else 0
+                shared_interleave(x_bf[:].unsqueeze(1), x_raw[a][:, :, lo:hi].unsqueeze(1), on_vector)
                 nc.vector.quantize_mx(
                     out=x_codes[a][:, lo:hi].bitcast(FP8X4),
                     scales=x_scales[4 * a : P, lo:hi],
@@ -122,34 +116,36 @@ def tile_picked_tome_lin_relu2_sub_e_kernel(tc, xT, w, b, gate, offs, out):
                 gather_codes(a, 0, S - DEFERRED, picked_tile(a, 0, S - DEFERRED, f"picked{a}"))
         nc.vector.tensor_copy(picked_scales[:], x_scales[:].indirect(offsets[:]))
 
-        w_scales = {0: reused.tile([P, D * N], U8, name="w_scales0", align_bytes=64, offset=0)[:]}
-        picked_last = reused.tile([P, S], U32, name="picked_last", align_bytes=64, offset=1024)
-        later_scales = reused.tile([P, LAST * D * N], U8, name="later_scales", align_bytes=64, offset=5120)
-        for c in range(1, PASSES):
-            w_scales[c] = later_scales[:, (c - 1) * D * N : c * D * N]
-        gpsimd_bf = keep.tile([P, 4, N, PACK], BF16, name="gpsimd_bf", tag="ring", align_bytes=64)
-        for i, (a, lo, hi) in enumerate(W_LOADS):
-            if i in W_GPSIMD:
-                k = 2 * W_GPSIMD.index(i)
-                w_bf = gpsimd_bf[:, k : k + 2, :, :]
-                nc.gpsimd.tensor_scalar(
-                    out=w_bf, in0=w_raw[i][:].rearrange("p d j m -> p d m j"), scalar1=1.0, scalar2=0.0, op0=ALU.mult, op1=ALU.add
-                )
-            else:
-                if i in W_VECTOR:
-                    w_bf = reused.tile([P, hi - lo, N, PACK], BF16, name=f"w_bf{i}", align_bytes=64, offset=7680)[:]
-                else:
-                    w_bf = keep.tile([P, hi - lo, N, PACK], BF16, name=f"w_bf{i}", align_bytes=64)[:]
-                shared_interleave(w_bf, w_raw[i][:], W_VECTOR.get(i, 0))
+        all_w_scales = reused.tile([P, PASSES * D * N], U8, name="w_scales", align_bytes=64, offset=5120)
+        w_scales = [all_w_scales[:, a * D * N : (a + 1) * D * N] for a in range(PASSES)]
+
+        def quantize_w(a, lo, hi, w_bf):
             cols = slice(lo * N, hi * N)
             nc.vector.quantize_mx(
                 out=w_codes[a][:, cols].bitcast(FP8X4),
                 scales=w_scales[a][:, cols],
                 in_=w_bf.rearrange("p d m j -> p (d m j)"),
             )
+
+        for i, (a, lo, hi) in enumerate(W_LOADS):
+            if i == 0:
+                w_bf = keep.tile([P, hi - lo, N, PACK], BF16, name=f"w_bf{i}", tag="ring", align_bytes=64)
+                nc.gpsimd.tensor_scalar(
+                    out=w_bf[:], in0=w_raw[i][:].rearrange("p d j m -> p d m j"), scalar1=1.0, scalar2=0.0, op0=ALU.mult, op1=ALU.add
+                )
+                quantize_w(a, 0, 2, w_bf[:, 0:2, :, :])
+                quantize_w(a, 2, 3, w_bf[:, 2:3, :, :])
+            else:
+                if i in W_VECTOR:
+                    w_bf = reused.tile([P, hi - lo, N, PACK], BF16, name=f"w_bf{i}", align_bytes=64, offset=RAW_AT[i - 2])
+                else:
+                    w_bf = keep.tile([P, hi - lo, N, PACK], BF16, name=f"w_bf{i}", align_bytes=64)
+                shared_interleave(w_bf[:], w_raw[i][:], W_VECTOR.get(i, 0))
+                quantize_w(a, lo, hi, w_bf[:])
             if i in GATHER_AFTER:
-                c = GATHER_AFTER[i]
-                gather_codes(LAST, c * V, (c + 1) * V, picked_last[:, c * V : (c + 1) * V])
+                first, end = GATHER_AFTER[i]
+                dst = reused.tile([P, (end - first) * V], U32, name=f"picked_last{first}", align_bytes=64, offset=PICKED_AT[i])
+                gather_codes(LAST, first * V, end * V, dst[:])
             for d in range(lo, hi):
                 for h in range(2):
                     s = d * V + h * VH

@@ -26,13 +26,16 @@ VH = V // 2
 RUN = 4
 
 X_PIECES = ((0, 256), (256, 768), (768, 1024))
+X_LAST_PIECES = ((0, 512), (512, 768), (768, 1024))
+X_LAST_VECTOR = 64
 X_VECTOR_FIRST, X_VECTOR_STEP = 512, 56
-DEFERRED = 256
+DEFERRED = 128
+CODE_WINDOW = 1216
 W_LOADS = ((0, 0, 3), (0, 3, 4), (1, 0, 2), (1, 2, 4)) + tuple((a, d, d + 1) for a in (2, 3) for d in range(D))
 W_VECTOR = {11: 64}
-GATHER_AFTER = {3: (0, 1), 5: (1, 2), 8: (2, 4)}
-RAW_AT = {3: 0, 0: 4096, 5: 10240, 8: 12288, 9: 14336}
-PICKED_AT = {3: 3584, 5: 9728, 8: 12288}
+GATHER_AFTER = {3: (0, 1), 5: (1, 2), 6: (2, 3), 8: (3, 4)}
+RAW_AT = {3: 0, 0: 4096, 5: 10240, 6: 12288, 8: 14336, 9: 16384}
+PICKED_AT = {3: 3584, 5: 9728, 6: 12288, 8: 14336}
 
 
 def tile_picked_tome_lin_relu2_sub_e_kernel(tc, xT, w, b, gate, offs, out):
@@ -45,14 +48,15 @@ def tile_picked_tome_lin_relu2_sub_e_kernel(tc, xT, w, b, gate, offs, out):
         offsets = keep.tile([P, S // 16], U16, name="offsets")
         bias = keep.tile([P, 1], F32, name="bias")
         gates = keep.tile([P, S], F32, name="gates")
-        x_raw = [keep.tile([P, PACK, T], F32, name=f"x_raw{a}", tag=f"x_raw{a}", align_bytes=64) for a in range(PASSES)]
+        x_raw = [keep.tile([P, PACK, T], F32, name=f"x_raw{a}", tag=f"x_raw{a}", align_bytes=64) for a in range(LAST)]
+        x_last = [keep.tile([P, PACK, HALF], F32, name=f"x_last{c}", tag=f"x_last{c}", align_bytes=64) for c in range(2)]
         w_raw = []
         for i, (a, lo, hi) in enumerate(W_LOADS):
             if i in RAW_AT:
                 w_raw.append(reused.tile([P, hi - lo, PACK, N], F32, name=f"w_raw{i}", align_bytes=64, offset=RAW_AT[i]))
             else:
                 w_raw.append(keep.tile([P, hi - lo, PACK, N], F32, name=f"w_raw{i}", align_bytes=64))
-        x_codes = [keep.tile([P, T], U32, name=f"x_codes{a}", align_bytes=64) for a in range(PASSES)]
+        x_codes = [keep.tile([P, CODE_WINDOW if a < LAST else T], U32, name=f"x_codes{a}", align_bytes=64) for a in range(PASSES)]
         x_scales = keep.tile([P, X_WINDOW], U8, name="x_scales", align_bytes=64)
         picked_scales = keep.tile([P, S], U8, name="picked_scales", align_bytes=64)
         w_codes = [keep.tile([P, D * N], U32, name=f"w_codes{a}", align_bytes=64) for a in range(PASSES)]
@@ -64,7 +68,12 @@ def tile_picked_tome_lin_relu2_sub_e_kernel(tc, xT, w, b, gate, offs, out):
 
         for a in range(PASSES):
             src = xT[a * PASS_K : (a + 1) * PASS_K, :]
-            nc.sync.dma_start(out=x_raw[a][:], in_=src.rearrange("(p j) t -> p j t", j=PACK))
+            src = src.rearrange("(p j) t -> p j t", j=PACK)
+            if a < LAST:
+                nc.sync.dma_start(out=x_raw[a][:], in_=src)
+            else:
+                for c in range(2):
+                    nc.sync.dma_start(out=x_last[c][:], in_=src[:, :, c * HALF : (c + 1) * HALF])
             if a == 0:
                 nc.sync.dma_start(offsets[:], offs)
         for i, (a, lo, hi) in enumerate(W_LOADS):
@@ -75,6 +84,8 @@ def tile_picked_tome_lin_relu2_sub_e_kernel(tc, xT, w, b, gate, offs, out):
             nc.sync.dma_start(out=gates[:, c * HALF : (c + 1) * HALF], in_=gate[:, c * HALF : (c + 1) * HALF])
 
         nc.gpsimd.memset(x_scales[:], 0)
+        for a in range(LAST):
+            nc.gpsimd.memset(x_codes[a][:, T:CODE_WINDOW], 0)
 
         def interleave(copy, dst, src):
             copy(
@@ -95,23 +106,29 @@ def tile_picked_tome_lin_relu2_sub_e_kernel(tc, xT, w, b, gate, offs, out):
             return keep.tile([P, hi - lo], U32, name=f"picked{a}_{lo}", tag=tag, align_bytes=64)[:]
 
         def gather_codes(a, lo, hi, dst):
-            nc.vector.tensor_copy(dst, x_codes[a][:].indirect(offsets[:, lo // 16 : hi // 16]))
+            window = x_codes[a][:] if 4 * (hi - lo) > 3 * T else x_codes[a][:, 0:T]
+            nc.vector.tensor_copy(dst, window.indirect(offsets[:, lo // 16 : hi // 16]))
             for s in range(lo, hi, VH):
                 picked[a, s] = dst[:, s - lo : s - lo + VH]
 
         for a in range(PASSES):
-            for lo, hi in X_PIECES:
+            for lo, hi in X_PIECES if a < LAST else X_LAST_PIECES:
                 tag = "ring" if hi == T and a == LAST else f"x_bf{a}_{lo}"
                 x_bf = keep.tile([P, hi - lo, PACK], BF16, name=f"x_bf{a}_{lo}", tag=tag, align_bytes=64)
-                on_vector = X_VECTOR_FIRST - X_VECTOR_STEP * a if hi - lo == HALF else 0
-                shared_interleave(x_bf[:].unsqueeze(1), x_raw[a][:, :, lo:hi].unsqueeze(1), on_vector)
+                if a < LAST:
+                    on_vector = X_VECTOR_FIRST - X_VECTOR_STEP * a if hi - lo == HALF else 0
+                    raw = x_raw[a][:, :, lo:hi]
+                else:
+                    on_vector = X_LAST_VECTOR if lo == HALF else 0
+                    raw = x_last[lo // HALF][:, :, lo % HALF : lo % HALF + hi - lo]
+                shared_interleave(x_bf[:].unsqueeze(1), raw.unsqueeze(1), on_vector)
                 nc.vector.quantize_mx(
                     out=x_codes[a][:, lo:hi].bitcast(FP8X4),
                     scales=x_scales[4 * a : P, lo:hi],
                     in_=x_bf[:].rearrange("p t j -> p (t j)"),
                 )
             if a > 0:
-                gather_codes(a - 1, S - DEFERRED, S, picked_tile(a - 1, S - DEFERRED, S, f"x_raw{a}"))
+                gather_codes(a - 1, S - DEFERRED, S, picked_tile(a - 1, S - DEFERRED, S, f"x_raw{a}" if a < LAST else "x_last1"))
             if a < LAST:
                 gather_codes(a, 0, S - DEFERRED, picked_tile(a, 0, S - DEFERRED, f"picked{a}"))
         nc.vector.tensor_copy(picked_scales[:], x_scales[:].indirect(offsets[:]))

@@ -26,16 +26,17 @@ VH = V // 2
 RUN = 4
 
 X_PIECES = ((0, 256), (256, 768), (768, 1024))
-X_LAST_PIECES = ((0, 512), (512, 768), (768, 1024))
-X_LAST_VECTOR = 64
-X_VECTOR_FIRST, X_VECTOR_STEP = 512, 56
+X_VECTOR = (512, 448, 320, 320)
+X_GPSIMD = (0, 0, 128, 128)
 DEFERRED = 128
 CODE_WINDOW = 1216
-W_LOADS = ((0, 0, 3), (0, 3, 4), (1, 0, 2), (1, 2, 4)) + tuple((a, d, d + 1) for a in (2, 3) for d in range(D))
-W_VECTOR = {11: 64}
-GATHER_AFTER = {3: (0, 1), 5: (1, 2), 6: (2, 3), 8: (3, 4)}
-RAW_AT = {3: 0, 0: 4096, 5: 10240, 6: 12288, 8: 14336, 9: 16384}
-PICKED_AT = {3: 3584, 5: 9728, 6: 12288, 8: 14336}
+MATRICES = PASSES * D
+ON_GPSIMD = 3
+W_GROUPS = ((0, 2), (2, 3), (3, 7), (7, 11), (11, 13), (13, 14), (14, 15), (15, 16))
+W_TILES = ((0, 3), (3, 11), (11, 13), (13, 16))
+GATHER_AFTER = {6: (0, 2), 10: (2, 3), 12: (3, 4)}
+RAW_AT = {6: 0, 10: 8192}
+PICKED_AT = {6: 1024, 10: 7680}
 
 
 def tile_picked_tome_lin_relu2_sub_e_kernel(tc, xT, w, b, gate, offs, out):
@@ -48,18 +49,18 @@ def tile_picked_tome_lin_relu2_sub_e_kernel(tc, xT, w, b, gate, offs, out):
         offsets = keep.tile([P, S // 16], U16, name="offsets")
         bias = keep.tile([P, 1], F32, name="bias")
         gates = keep.tile([P, S], F32, name="gates")
-        x_raw = [keep.tile([P, PACK, T], F32, name=f"x_raw{a}", tag=f"x_raw{a}", align_bytes=64) for a in range(LAST)]
-        x_last = [keep.tile([P, PACK, HALF], F32, name=f"x_last{c}", tag=f"x_last{c}", align_bytes=64) for c in range(2)]
-        w_raw = []
-        for i, (a, lo, hi) in enumerate(W_LOADS):
-            if i in RAW_AT:
-                w_raw.append(reused.tile([P, hi - lo, PACK, N], F32, name=f"w_raw{i}", align_bytes=64, offset=RAW_AT[i]))
+        x_raw = [keep.tile([P, PACK, T], F32, name=f"x_raw{a}", tag=f"x_raw{a}", align_bytes=64) for a in range(PASSES)]
+        first_raw = reused.tile([P, ON_GPSIMD, PACK, N], F32, name="first_raw", align_bytes=64, offset=2048)
+        w_raw = {}
+        for m in range(ON_GPSIMD, MATRICES):
+            if m in RAW_AT:
+                w_raw[m] = reused.tile([P, PACK, N], F32, name=f"w_raw{m}", align_bytes=64, offset=RAW_AT[m])
             else:
-                w_raw.append(keep.tile([P, hi - lo, PACK, N], F32, name=f"w_raw{i}", align_bytes=64))
+                w_raw[m] = keep.tile([P, PACK, N], F32, name=f"w_raw{m}", tag=f"w_raw{m}", align_bytes=64)
         x_codes = [keep.tile([P, CODE_WINDOW if a < LAST else T], U32, name=f"x_codes{a}", align_bytes=64) for a in range(PASSES)]
         x_scales = keep.tile([P, X_WINDOW], U8, name="x_scales", align_bytes=64)
         picked_scales = keep.tile([P, S], U8, name="picked_scales", align_bytes=64)
-        w_codes = [keep.tile([P, D * N], U32, name=f"w_codes{a}", align_bytes=64) for a in range(PASSES)]
+        w_codes = keep.tile([P, MATRICES * N], U32, name="w_codes", align_bytes=64)
         r = keep.tile([P, V], F32, name="r")
         ug = keep.tile([P, V], F32, name="ug")
         y = keep.tile([P, D - 1, V], F32, name="y")
@@ -68,17 +69,14 @@ def tile_picked_tome_lin_relu2_sub_e_kernel(tc, xT, w, b, gate, offs, out):
 
         for a in range(PASSES):
             src = xT[a * PASS_K : (a + 1) * PASS_K, :]
-            src = src.rearrange("(p j) t -> p j t", j=PACK)
-            if a < LAST:
-                nc.sync.dma_start(out=x_raw[a][:], in_=src)
-            else:
-                for c in range(2):
-                    nc.sync.dma_start(out=x_last[c][:], in_=src[:, :, c * HALF : (c + 1) * HALF])
+            nc.sync.dma_start(out=x_raw[a][:], in_=src.rearrange("(p j) t -> p j t", j=PACK))
             if a == 0:
                 nc.sync.dma_start(offsets[:], offs)
-        for i, (a, lo, hi) in enumerate(W_LOADS):
-            src = w[lo:hi, a * PASS_K : (a + 1) * PASS_K, :].rearrange("d (p j) m -> p d j m", j=PACK)
-            nc.sync.dma_start(out=w_raw[i][:], in_=src)
+        nc.sync.dma_start(out=first_raw[:], in_=w[0:ON_GPSIMD, 0:PASS_K, :].rearrange("d (p j) m -> p d j m", j=PACK))
+        for m in range(ON_GPSIMD, MATRICES):
+            a, d = divmod(m, D)
+            src = w[d, a * PASS_K : (a + 1) * PASS_K, :]
+            nc.sync.dma_start(out=w_raw[m][:], in_=src.rearrange("(p j) m -> p j m", j=PACK))
         nc.sync.dma_start(out=bias[:], in_=b)
         for c in range(2):
             nc.sync.dma_start(out=gates[:, c * HALF : (c + 1) * HALF], in_=gate[:, c * HALF : (c + 1) * HALF])
@@ -112,68 +110,68 @@ def tile_picked_tome_lin_relu2_sub_e_kernel(tc, xT, w, b, gate, offs, out):
                 picked[a, s] = dst[:, s - lo : s - lo + VH]
 
         for a in range(PASSES):
-            for lo, hi in X_PIECES if a < LAST else X_LAST_PIECES:
-                tag = "ring" if hi == T and a == LAST else f"x_bf{a}_{lo}"
+            for lo, hi in X_PIECES:
+                tag = "ring" if hi == T and a > 0 else f"x_bf{a}_{lo}"
                 x_bf = keep.tile([P, hi - lo, PACK], BF16, name=f"x_bf{a}_{lo}", tag=tag, align_bytes=64)
-                if a < LAST:
-                    on_vector = X_VECTOR_FIRST - X_VECTOR_STEP * a if hi - lo == HALF else 0
-                    raw = x_raw[a][:, :, lo:hi]
-                else:
-                    on_vector = X_LAST_VECTOR if lo == HALF else 0
-                    raw = x_last[lo // HALF][:, :, lo % HALF : lo % HALF + hi - lo]
-                shared_interleave(x_bf[:].unsqueeze(1), raw.unsqueeze(1), on_vector)
+                on_vector = X_VECTOR[a] if hi - lo == HALF else 0
+                mid = hi - X_GPSIMD[a] if hi == T else hi
+                shared_interleave(x_bf[:, 0 : mid - lo, :].unsqueeze(1), x_raw[a][:, :, lo:mid].unsqueeze(1), on_vector)
+                if mid < hi:
+                    nc.gpsimd.tensor_copy(out=x_bf[:, mid - lo : hi - lo, :], in_=x_raw[a][:, :, mid:hi].rearrange("p j t -> p t j"))
                 nc.vector.quantize_mx(
                     out=x_codes[a][:, lo:hi].bitcast(FP8X4),
                     scales=x_scales[4 * a : P, lo:hi],
                     in_=x_bf[:].rearrange("p t j -> p (t j)"),
                 )
             if a > 0:
-                gather_codes(a - 1, S - DEFERRED, S, picked_tile(a - 1, S - DEFERRED, S, f"x_raw{a}" if a < LAST else "x_last1"))
+                gather_codes(a - 1, S - DEFERRED, S, picked_tile(a - 1, S - DEFERRED, S, f"x_raw{a}"))
             if a < LAST:
                 gather_codes(a, 0, S - DEFERRED, picked_tile(a, 0, S - DEFERRED, f"picked{a}"))
         nc.vector.tensor_copy(picked_scales[:], x_scales[:].indirect(offsets[:]))
 
-        all_w_scales = reused.tile([P, PASSES * D * N], U8, name="w_scales", align_bytes=64, offset=5120)
-        w_scales = [all_w_scales[:, a * D * N : (a + 1) * D * N] for a in range(PASSES)]
+        w_scales = reused.tile([P, MATRICES * N], U8, name="w_scales", align_bytes=64, offset=3072)
+        first_bf = keep.tile([P, ON_GPSIMD, N, PACK], BF16, name="first_bf", tag="ring", align_bytes=64)
+        w_bf = [
+            first_bf,
+            keep.tile([P, 8, N, PACK], BF16, name="early_bf", align_bytes=64),
+            reused.tile([P, 2, N, PACK], BF16, name="late_bf", align_bytes=64, offset=5120),
+            keep.tile([P, 3, N, PACK], BF16, name="last_bf", tag="w_raw11", align_bytes=64),
+        ]
 
-        def quantize_w(a, lo, hi, w_bf):
-            cols = slice(lo * N, hi * N)
+        def rounded(lo, hi):
+            i = [i for i, (first, end) in enumerate(W_TILES) if first <= lo < end][0]
+            return w_bf[i][:, lo - W_TILES[i][0] : hi - W_TILES[i][0], :, :]
+
+        nc.gpsimd.tensor_scalar(
+            out=first_bf[:], in0=first_raw[:].rearrange("p d j m -> p d m j"), scalar1=1.0, scalar2=0.0, op0=ALU.mult, op1=ALU.add
+        )
+        for lo, hi in W_GROUPS:
+            for m in range(max(lo, ON_GPSIMD), hi):
+                interleave(nc.scalar.copy, rounded(m, m + 1), w_raw[m][:].unsqueeze(1))
             nc.vector.quantize_mx(
-                out=w_codes[a][:, cols].bitcast(FP8X4),
-                scales=w_scales[a][:, cols],
-                in_=w_bf.rearrange("p d m j -> p (d m j)"),
+                out=w_codes[:, lo * N : hi * N].bitcast(FP8X4),
+                scales=w_scales[:, lo * N : hi * N],
+                in_=rounded(lo, hi).rearrange("p d m j -> p (d m j)"),
             )
-
-        for i, (a, lo, hi) in enumerate(W_LOADS):
-            if i == 0:
-                w_bf = keep.tile([P, hi - lo, N, PACK], BF16, name=f"w_bf{i}", tag="ring", align_bytes=64)
-                nc.gpsimd.tensor_scalar(
-                    out=w_bf[:], in0=w_raw[i][:].rearrange("p d j m -> p d m j"), scalar1=1.0, scalar2=0.0, op0=ALU.mult, op1=ALU.add
-                )
-                quantize_w(a, 0, 2, w_bf[:, 0:2, :, :])
-                quantize_w(a, 2, 3, w_bf[:, 2:3, :, :])
-            else:
-                if i in W_VECTOR:
-                    w_bf = reused.tile([P, hi - lo, N, PACK], BF16, name=f"w_bf{i}", align_bytes=64, offset=RAW_AT[i - 2])
+            if hi - 1 in GATHER_AFTER:
+                first, end = GATHER_AFTER[hi - 1]
+                if hi - 1 in PICKED_AT:
+                    dst = reused.tile([P, (end - first) * V], U32, name=f"picked_last{first}", align_bytes=64, offset=PICKED_AT[hi - 1])[:]
                 else:
-                    w_bf = keep.tile([P, hi - lo, N, PACK], BF16, name=f"w_bf{i}", align_bytes=64)
-                shared_interleave(w_bf[:], w_raw[i][:], W_VECTOR.get(i, 0))
-                quantize_w(a, lo, hi, w_bf[:])
-            if i in GATHER_AFTER:
-                first, end = GATHER_AFTER[i]
-                dst = reused.tile([P, (end - first) * V], U32, name=f"picked_last{first}", align_bytes=64, offset=PICKED_AT[i])
-                gather_codes(LAST, first * V, end * V, dst[:])
-            for d in range(lo, hi):
+                    dst = picked_tile(LAST, first * V, end * V, f"w_raw{hi - 1}")
+                gather_codes(LAST, first * V, end * V, dst)
+            for m in range(lo, hi):
+                a, d = divmod(m, D)
                 for h in range(2):
                     s = d * V + h * VH
                     nc.tensor.matmul_mx(
                         out=acc[h][:],
-                        lhsT=w_codes[a][:, d * N : (d + 1) * N].bitcast(FP8X4),
-                        lhsT_scale=w_scales[a][:, d * N : (d + 1) * N],
+                        lhsT=w_codes[:, m * N : (m + 1) * N].bitcast(FP8X4),
+                        lhsT_scale=w_scales[:, m * N : (m + 1) * N],
                         rhs=picked[a, s].bitcast(FP8X4),
                         rhs_scale=picked_scales[4 * a : P, s : s + VH],
-                        start=(a == 0 and d == 0),
-                        stop=(a == LAST and d == D - 1),
+                        start=(m == 0),
+                        stop=(m == MATRICES - 1),
                     )
 
         halves = [slice(0, VH), slice(VH, V)]

@@ -25,9 +25,8 @@ OUT_WINDOW = 2048
 VH = V // 2
 RUN = 4
 
-X_PIECES = ((0, 256), (256, 768), (768, 1024))
-X_VECTOR = (512, 448, 320, 320)
-X_GPSIMD = (0, 0, 128, 128)
+BACK = 768
+X_VECTOR = (512, 448, 400, 384)
 DEFERRED = 128
 CODE_WINDOW = 1216
 MATRICES = PASSES * D
@@ -110,18 +109,15 @@ def tile_picked_tome_lin_relu2_sub_e_kernel(tc, xT, w, b, gate, offs, out):
                 picked[a, s] = dst[:, s - lo : s - lo + VH]
 
         for a in range(PASSES):
-            for lo, hi in X_PIECES:
-                tag = "ring" if hi == T and a > 0 else f"x_bf{a}_{lo}"
-                x_bf = keep.tile([P, hi - lo, PACK], BF16, name=f"x_bf{a}_{lo}", tag=tag, align_bytes=64)
-                on_vector = X_VECTOR[a] if hi - lo == HALF else 0
-                mid = hi - X_GPSIMD[a] if hi == T else hi
-                shared_interleave(x_bf[:, 0 : mid - lo, :].unsqueeze(1), x_raw[a][:, :, lo:mid].unsqueeze(1), on_vector)
-                if mid < hi:
-                    nc.gpsimd.tensor_copy(out=x_bf[:, mid - lo : hi - lo, :], in_=x_raw[a][:, :, mid:hi].rearrange("p j t -> p t j"))
+            front = keep.tile([P, BACK, PACK], BF16, name=f"x_front{a}", align_bytes=64)
+            back = keep.tile([P, T - BACK, PACK], BF16, name=f"x_back{a}", tag="ring" if a == LAST else f"x_back{a}", align_bytes=64)
+            shared_interleave(front[:].unsqueeze(1), x_raw[a][:, :, 0:BACK].unsqueeze(1), X_VECTOR[a])
+            interleave(nc.scalar.copy, back[:].unsqueeze(1), x_raw[a][:, :, BACK:T].unsqueeze(1))
+            for lo, hi, x_bf in ((HALF, BACK, front[:, HALF:BACK, :]), (0, HALF, front[:, 0:HALF, :]), (BACK, T, back[:])):
                 nc.vector.quantize_mx(
                     out=x_codes[a][:, lo:hi].bitcast(FP8X4),
                     scales=x_scales[4 * a : P, lo:hi],
-                    in_=x_bf[:].rearrange("p t j -> p (t j)"),
+                    in_=x_bf.rearrange("p t j -> p (t j)"),
                 )
             if a > 0:
                 gather_codes(a - 1, S - DEFERRED, S, picked_tile(a - 1, S - DEFERRED, S, f"x_raw{a}"))

@@ -31,11 +31,11 @@ DEFERRED = 128
 CODE_WINDOW = 1216
 MATRICES = PASSES * D
 ON_GPSIMD = 3
-W_GROUPS = ((0, 2), (2, 3), (3, 7), (7, 11), (11, 13), (13, 14), (14, 15), (15, 16))
-W_TILES = ((0, 3), (3, 11), (11, 13), (13, 16))
-GATHER_AFTER = {6: (0, 2), 10: (2, 3), 12: (3, 4)}
-RAW_AT = {6: 0, 10: 8192}
-PICKED_AT = {6: 1024, 10: 7680}
+SECOND = 7
+W_GROUPS = ((0, 2), (2, 3), (3, 7), (8, 12), (7, 8), (12, 14), (14, 15), (15, 16))
+GATHER_AFTER = {6: (0, 2), 7: (2, 3), 13: (3, 4)}
+RAW_AT = {6: 0, 7: 10240, 11: 12288}
+PICKED_AT = {6: 1024, 7: 11776}
 
 
 def tile_picked_tome_lin_relu2_sub_e_kernel(tc, xT, w, b, gate, offs, out):
@@ -127,23 +127,31 @@ def tile_picked_tome_lin_relu2_sub_e_kernel(tc, xT, w, b, gate, offs, out):
 
         w_scales = reused.tile([P, MATRICES * N], U8, name="w_scales", align_bytes=64, offset=3072)
         first_bf = keep.tile([P, ON_GPSIMD, N, PACK], BF16, name="first_bf", tag="ring", align_bytes=64)
-        w_bf = [
-            first_bf,
-            keep.tile([P, 8, N, PACK], BF16, name="early_bf", align_bytes=64),
-            reused.tile([P, 2, N, PACK], BF16, name="late_bf", align_bytes=64, offset=5120),
-            keep.tile([P, 3, N, PACK], BF16, name="last_bf", tag="w_raw11", align_bytes=64),
-        ]
+        w_bf = {
+            0: first_bf,
+            3: keep.tile([P, 4, N, PACK], BF16, name="w_bf3", tag="second_ring", align_bytes=64),
+            7: keep.tile([P, 1, N, PACK], BF16, name="w_bf7", tag="second_ring", align_bytes=64),
+            8: keep.tile([P, 4, N, PACK], BF16, name="w_bf8", align_bytes=64),
+            12: reused.tile([P, 2, N, PACK], BF16, name="w_bf12", align_bytes=64, offset=9216),
+            14: keep.tile([P, 2, N, PACK], BF16, name="w_bf14", tag="w_raw12", align_bytes=64),
+        }
 
         def rounded(lo, hi):
-            i = [i for i, (first, end) in enumerate(W_TILES) if first <= lo < end][0]
-            return w_bf[i][:, lo - W_TILES[i][0] : hi - W_TILES[i][0], :, :]
+            first = max(m for m in w_bf if m <= lo)
+            return w_bf[first][:, lo - first : hi - first, :, :]
 
-        nc.gpsimd.tensor_scalar(
-            out=first_bf[:], in0=first_raw[:].rearrange("p d j m -> p d m j"), scalar1=1.0, scalar2=0.0, op0=ALU.mult, op1=ALU.add
-        )
+        def gpsimd_interleave(dst, src):
+            nc.gpsimd.tensor_scalar(
+                out=dst, in0=src.rearrange("p d j m -> p d m j"), scalar1=1.0, scalar2=0.0, op0=ALU.mult, op1=ALU.add
+            )
+
+        gpsimd_interleave(first_bf[:], first_raw[:])
         for lo, hi in W_GROUPS:
             for m in range(max(lo, ON_GPSIMD), hi):
-                interleave(nc.scalar.copy, rounded(m, m + 1), w_raw[m][:].unsqueeze(1))
+                if m == SECOND:
+                    gpsimd_interleave(rounded(m, m + 1), w_raw[m][:].unsqueeze(1))
+                else:
+                    interleave(nc.scalar.copy, rounded(m, m + 1), w_raw[m][:].unsqueeze(1))
             nc.vector.quantize_mx(
                 out=w_codes[:, lo * N : hi * N].bitcast(FP8X4),
                 scales=w_scales[:, lo * N : hi * N],

@@ -33,7 +33,7 @@ MATRICES = PASSES * D
 ON_GPSIMD = 3
 SECOND = 7
 W_GROUPS = ((0, 2), (2, 3), (3, 7), (8, 12), (7, 8), (12, 14), (14, 15), (15, 16))
-GATHER_AFTER = {6: (0, 2), 7: (2, 3), 13: (3, 4)}
+GATHER_AFTER = {6: (1, 3), 7: (3, 4)}
 RAW_AT = {6: 0, 7: 10240, 11: 12288}
 PICKED_AT = {6: 1024, 7: 11776}
 
@@ -124,16 +124,23 @@ def tile_picked_tome_lin_relu2_sub_e_kernel(tc, xT, w, b, gate, offs, out):
             if a < LAST:
                 gather_codes(a, 0, S - DEFERRED, picked_tile(a, 0, S - DEFERRED, f"picked{a}"))
         nc.vector.tensor_copy(picked_scales[:], x_scales[:].indirect(offsets[:]))
+        gather_codes(LAST, 0, V, picked_tile(LAST, 0, V, "picked_last0"))
 
-        w_scales = reused.tile([P, MATRICES * N], U8, name="w_scales", align_bytes=64, offset=3072)
+        early_scales = reused.tile([P, LAST * D * N], U8, name="early_scales", align_bytes=64, offset=3072)
+        late_scales = reused.tile([P, D * N], U8, name="late_scales", align_bytes=64, offset=RAW_AT[SECOND])
+
+        def w_scales(lo, hi):
+            if lo < LAST * D:
+                return early_scales[:, lo * N : hi * N]
+            return late_scales[:, (lo - LAST * D) * N : (hi - LAST * D) * N]
+
         first_bf = keep.tile([P, ON_GPSIMD, N, PACK], BF16, name="first_bf", tag="ring", align_bytes=64)
         w_bf = {
             0: first_bf,
             3: keep.tile([P, 4, N, PACK], BF16, name="w_bf3", tag="second_ring", align_bytes=64),
             7: keep.tile([P, 1, N, PACK], BF16, name="w_bf7", tag="second_ring", align_bytes=64),
             8: keep.tile([P, 4, N, PACK], BF16, name="w_bf8", align_bytes=64),
-            12: reused.tile([P, 2, N, PACK], BF16, name="w_bf12", align_bytes=64, offset=9216),
-            14: keep.tile([P, 2, N, PACK], BF16, name="w_bf14", tag="w_raw12", align_bytes=64),
+            12: keep.tile([P, 4, N, PACK], BF16, name="w_bf12", align_bytes=64),
         }
 
         def rounded(lo, hi):
@@ -154,7 +161,7 @@ def tile_picked_tome_lin_relu2_sub_e_kernel(tc, xT, w, b, gate, offs, out):
                     interleave(nc.scalar.copy, rounded(m, m + 1), w_raw[m][:].unsqueeze(1))
             nc.vector.quantize_mx(
                 out=w_codes[:, lo * N : hi * N].bitcast(FP8X4),
-                scales=w_scales[:, lo * N : hi * N],
+                scales=w_scales(lo, hi),
                 in_=rounded(lo, hi).rearrange("p d m j -> p (d m j)"),
             )
             if hi - 1 in GATHER_AFTER:
@@ -171,7 +178,7 @@ def tile_picked_tome_lin_relu2_sub_e_kernel(tc, xT, w, b, gate, offs, out):
                     nc.tensor.matmul_mx(
                         out=acc[h][:],
                         lhsT=w_codes[:, m * N : (m + 1) * N].bitcast(FP8X4),
-                        lhsT_scale=w_scales[:, m * N : (m + 1) * N],
+                        lhsT_scale=w_scales(m, m + 1),
                         rhs=picked[a, s].bitcast(FP8X4),
                         rhs_scale=picked_scales[4 * a : P, s : s + VH],
                         start=(m == 0),

@@ -21,7 +21,7 @@ PASSES = K // PASS_K
 LAST = PASSES - 1
 HALF = T // 2
 X_WINDOW = 1408
-OUT_WINDOW = 2048
+STORES = (512, 512)
 VH = V // 2
 RUN = 4
 
@@ -60,10 +60,7 @@ def tile_picked_tome_lin_relu2_sub_e_kernel(tc, xT, w, b, gate, offs, out):
         x_scales = keep.tile([P, X_WINDOW], U8, name="x_scales", align_bytes=64)
         picked_scales = keep.tile([P, S], U8, name="picked_scales", align_bytes=64)
         w_codes = keep.tile([P, MATRICES * N], U32, name="w_codes", align_bytes=64)
-        r = keep.tile([P, V], F32, name="r")
-        ug = keep.tile([P, V], F32, name="ug")
-        y = keep.tile([P, D - 1, V], F32, name="y")
-        result = keep.tile([P, OUT_WINDOW], F32, name="result")
+        windows = [keep.tile([P, T], F32, name=f"window{e}") for e in range(2)]
         acc = [psum.tile([P, VH], F32, name=f"acc{h}") for h in range(2)]
 
         for a in range(PASSES):
@@ -77,12 +74,14 @@ def tile_picked_tome_lin_relu2_sub_e_kernel(tc, xT, w, b, gate, offs, out):
             src = w[d, a * PASS_K : (a + 1) * PASS_K, :]
             nc.sync.dma_start(out=w_raw[m][:], in_=src.rearrange("(p j) m -> p j m", j=PACK))
         nc.sync.dma_start(out=bias[:], in_=b)
-        for c in range(2):
+        for c in (1, 0):
             nc.sync.dma_start(out=gates[:, c * HALF : (c + 1) * HALF], in_=gate[:, c * HALF : (c + 1) * HALF])
 
         nc.gpsimd.memset(x_scales[:], 0)
         for a in range(LAST):
             nc.gpsimd.memset(x_codes[a][:, T:CODE_WINDOW], 0)
+        for window in windows:
+            nc.gpsimd.memset(window[:], 0.0)
 
         def interleave(copy, dst, src):
             copy(
@@ -185,16 +184,28 @@ def tile_picked_tome_lin_relu2_sub_e_kernel(tc, xT, w, b, gate, offs, out):
                         stop=(m == MATRICES - 1),
                     )
 
-        halves = [slice(0, VH), slice(VH, V)]
-        nc.scalar.activation(out=r[:, halves[0]], in_=acc[0][:], func=ACT.Relu, bias=bias[:, 0:1])
-        nc.vector.tensor_scalar(out=r[:, halves[1]], in0=acc[1][:], scalar1=bias[:, 0:1], scalar2=0.0, op0=ALU.add, op1=ALU.max)
-        for h in (1, 0):
-            nc.vector.scalar_tensor_tensor(
-                out=ug[:, halves[h]], in0=acc[h][:], scalar=bias[:, 0:1], in1=gates[:, halves[h]], op0=ALU.add, op1=ALU.mult
+        r = keep.tile([P, V], F32, name="r")
+        y = keep.tile([P, V], F32, name="y")
+        weighted = keep.tile([P, S // 2], F32, name="weighted")
+        nc.scalar.activation(out=r[:, 0:VH], in_=acc[0][:], func=ACT.Relu, bias=bias[:, 0:1])
+        nc.vector.tensor_scalar(out=r[:, VH:V], in0=acc[1][:], scalar1=bias[:, 0:1], scalar2=0.0, op0=ALU.add, op1=ALU.max)
+        for h in range(2):
+            nc.scalar.activation(out=y[:, h * VH : (h + 1) * VH], in_=r[:, h * VH : (h + 1) * VH], func=ACT.Square)
+        base = S // 2
+        for lo, hi in ((0, VH), (VH, V), (V, 2 * V)):
+            nc.vector.tensor_tensor(weighted[:, lo:hi], y[:, lo % V : lo % V + hi - lo], gates[:, base + lo : base + hi], ALU.mult)
+        for lo, hi in ((0, VH), (VH, 2 * V)):
+            nc.scalar.activation(
+                out=windows[1][:].indirect(offsets[:, (base + lo) // 16 : (base + hi) // 16]), in_=weighted[:, lo:hi], func=ACT.Copy
             )
-        nc.scalar.activation(out=y[:], in_=r[:].unsqueeze(1).to_broadcast([P, D - 1, V]), func=ACT.Square)
-        nc.vector.tensor_tensor(result[:].indirect(offsets[:, 0 : V // 16]), r[:], ug[:], ALU.mult)
-        nc.vector.tensor_tensor(
-            result[:].indirect(offsets[:, V // 16 : S // 16]), y[:].rearrange("p d v -> p (d v)"), gates[:, V:S], ALU.mult
-        )
-        nc.sync.dma_start(out=out, in_=result[:, 0:T])
+        for d in range(2):
+            nc.vector.tensor_tensor(
+                windows[0][:].indirect(offsets[:, d * V // 16 : (d + 1) * V // 16]), y[:], gates[:, d * V : (d + 1) * V], ALU.mult
+            )
+        result = keep.tile([P, T], F32, name="result")
+        lo = 0
+        for width in STORES:
+            cols = slice(lo, lo + width)
+            nc.vector.tensor_tensor(result[:, cols], windows[0][:, cols], windows[1][:, cols], ALU.add)
+            nc.sync.dma_start(out=out[:, cols], in_=result[:, cols])
+            lo = lo + width

@@ -185,23 +185,26 @@ def tile_picked_tome_lin_relu2_sub_e_kernel(tc, xT, w, b, gate, offs, out):
                     )
 
         r = keep.tile([P, V], F32, name="r")
-        y = keep.tile([P, V], F32, name="y")
+        y = keep.tile([P, 2 * V], F32, name="y")
         weighted = keep.tile([P, S // 2], F32, name="weighted")
-        nc.scalar.activation(out=r[:, 0:VH], in_=acc[0][:], func=ACT.Relu, bias=bias[:, 0:1])
-        nc.vector.tensor_scalar(out=r[:, VH:V], in0=acc[1][:], scalar1=bias[:, 0:1], scalar2=0.0, op0=ALU.add, op1=ALU.max)
-        for h in range(2):
-            nc.scalar.activation(out=y[:, h * VH : (h + 1) * VH], in_=r[:, h * VH : (h + 1) * VH], func=ACT.Square)
+        lifted = keep.tile([P, VH], F32, name="lifted")
         base = S // 2
-        for lo, hi in ((0, VH), (VH, V), (V, 2 * V)):
+        nc.vector.tensor_scalar(out=r[:, 0:VH], in0=acc[0][:], scalar1=bias[:, 0:1], scalar2=0.0, op0=ALU.add, op1=ALU.max)
+        nc.vector.scalar_tensor_tensor(
+            out=lifted[:], in0=acc[0][:], scalar=bias[:, 0:1], in1=gates[:, base : base + VH], op0=ALU.add, op1=ALU.mult
+        )
+        nc.scalar.activation(out=r[:, VH:V], in_=acc[1][:], func=ACT.Relu, bias=bias[:, 0:1])
+        nc.vector.tensor_tensor(weighted[:, 0:VH], r[:, 0:VH], lifted[:], ALU.mult)
+        for h in (1, 0):
+            nc.scalar.activation(out=y[:, h * VH : (h + 1) * VH], in_=r[:, h * VH : (h + 1) * VH], func=ACT.Square)
+        nc.scalar.activation(out=y[:, V : 2 * V], in_=r[:], func=ACT.Square)
+        for lo, hi in ((VH, V), (V, 2 * V)):
             nc.vector.tensor_tensor(weighted[:, lo:hi], y[:, lo % V : lo % V + hi - lo], gates[:, base + lo : base + hi], ALU.mult)
         for lo, hi in ((0, VH), (VH, 2 * V)):
             nc.scalar.activation(
                 out=windows[1][:].indirect(offsets[:, (base + lo) // 16 : (base + hi) // 16]), in_=weighted[:, lo:hi], func=ACT.Copy
             )
-        for d in range(2):
-            nc.vector.tensor_tensor(
-                windows[0][:].indirect(offsets[:, d * V // 16 : (d + 1) * V // 16]), y[:], gates[:, d * V : (d + 1) * V], ALU.mult
-            )
+        nc.vector.tensor_tensor(windows[0][:].indirect(offsets[:, 0 : base // 16]), y[:], gates[:, 0:base], ALU.mult)
         result = keep.tile([P, T], F32, name="result")
         lo = 0
         for width in STORES:

@@ -21,12 +21,12 @@ PASSES = K // PASS_K
 LAST = PASSES - 1
 HALF = T // 2
 X_WINDOW = 1408
-STORES = (512, 512)
+STORES = (384, 384, 256)
 VH = V // 2
 RUN = 4
 
 BACK = 768
-X_VECTOR = (512, 448, 400, 384)
+X_VECTOR = (512, 448, 400, 160)
 DEFERRED = 128
 CODE_WINDOW = 1216
 MATRICES = PASSES * D
@@ -48,14 +48,16 @@ def tile_picked_tome_lin_relu2_sub_e_kernel(tc, xT, w, b, gate, offs, out):
         offsets = keep.tile([P, S // 16], U16, name="offsets")
         bias = keep.tile([P, 1], F32, name="bias")
         gates = keep.tile([P, S], F32, name="gates")
-        x_raw = [keep.tile([P, PACK, T], F32, name=f"x_raw{a}", tag=f"x_raw{a}", align_bytes=64) for a in range(PASSES)]
-        first_raw = reused.tile([P, ON_GPSIMD, PACK, N], F32, name="first_raw", align_bytes=64, offset=2048)
-        w_raw = {}
-        for m in range(ON_GPSIMD, MATRICES):
+        x_raw = [keep.tile([P, PACK, T], F32, name=f"x_raw{a}", tag=f"x_raw{a}", align_bytes=64) for a in range(LAST)]
+        last_raw = [keep.tile([P, PACK, HALF], F32, name=f"last_raw{c}", tag=f"last_raw{c}", align_bytes=64) for c in range(2)]
+        first_raw = reused.tile([P, D, PACK, N], F32, name="first_raw", align_bytes=64, offset=2048)
+        pair_raw = keep.tile([P, 2, PACK, N], F32, name="pair_raw", align_bytes=64)
+        w_raw = {ON_GPSIMD: first_raw[:, ON_GPSIMD], D: pair_raw[:, 0], D + 1: pair_raw[:, 1]}
+        for m in range(D + 2, MATRICES):
             if m in RAW_AT:
-                w_raw[m] = reused.tile([P, PACK, N], F32, name=f"w_raw{m}", align_bytes=64, offset=RAW_AT[m])
+                w_raw[m] = reused.tile([P, PACK, N], F32, name=f"w_raw{m}", align_bytes=64, offset=RAW_AT[m])[:]
             else:
-                w_raw[m] = keep.tile([P, PACK, N], F32, name=f"w_raw{m}", tag=f"w_raw{m}", align_bytes=64)
+                w_raw[m] = keep.tile([P, PACK, N], F32, name=f"w_raw{m}", tag=f"w_raw{m}", align_bytes=64)[:]
         x_codes = [keep.tile([P, CODE_WINDOW if a < LAST else T], U32, name=f"x_codes{a}", align_bytes=64) for a in range(PASSES)]
         x_scales = keep.tile([P, X_WINDOW], U8, name="x_scales", align_bytes=64)
         picked_scales = keep.tile([P, S], U8, name="picked_scales", align_bytes=64)
@@ -65,14 +67,19 @@ def tile_picked_tome_lin_relu2_sub_e_kernel(tc, xT, w, b, gate, offs, out):
 
         for a in range(PASSES):
             src = xT[a * PASS_K : (a + 1) * PASS_K, :]
-            nc.sync.dma_start(out=x_raw[a][:], in_=src.rearrange("(p j) t -> p j t", j=PACK))
+            if a < LAST:
+                nc.sync.dma_start(out=x_raw[a][:], in_=src.rearrange("(p j) t -> p j t", j=PACK))
+            else:
+                for c in range(2):
+                    nc.sync.dma_start(out=last_raw[c][:], in_=src[:, c * HALF : (c + 1) * HALF].rearrange("(p j) t -> p j t", j=PACK))
             if a == 0:
                 nc.sync.dma_start(offsets[:], offs)
-        nc.sync.dma_start(out=first_raw[:], in_=w[0:ON_GPSIMD, 0:PASS_K, :].rearrange("d (p j) m -> p d j m", j=PACK))
-        for m in range(ON_GPSIMD, MATRICES):
+        nc.sync.dma_start(out=first_raw[:], in_=w[:, 0:PASS_K, :].rearrange("d (p j) m -> p d j m", j=PACK))
+        nc.sync.dma_start(out=pair_raw[:], in_=w[0:2, PASS_K : 2 * PASS_K, :].rearrange("d (p j) m -> p d j m", j=PACK))
+        for m in range(D + 2, MATRICES):
             a, d = divmod(m, D)
             src = w[d, a * PASS_K : (a + 1) * PASS_K, :]
-            nc.sync.dma_start(out=w_raw[m][:], in_=src.rearrange("(p j) m -> p j m", j=PACK))
+            nc.sync.dma_start(out=w_raw[m], in_=src.rearrange("(p j) m -> p j m", j=PACK))
         nc.sync.dma_start(out=bias[:], in_=b)
         for c in (1, 0):
             nc.sync.dma_start(out=gates[:, c * HALF : (c + 1) * HALF], in_=gate[:, c * HALF : (c + 1) * HALF])
@@ -110,16 +117,23 @@ def tile_picked_tome_lin_relu2_sub_e_kernel(tc, xT, w, b, gate, offs, out):
         for a in range(PASSES):
             front = keep.tile([P, BACK, PACK], BF16, name=f"x_front{a}", align_bytes=64)
             back = keep.tile([P, T - BACK, PACK], BF16, name=f"x_back{a}", tag="ring" if a == LAST else f"x_back{a}", align_bytes=64)
-            shared_interleave(front[:].unsqueeze(1), x_raw[a][:, :, 0:BACK].unsqueeze(1), X_VECTOR[a])
-            interleave(nc.scalar.copy, back[:].unsqueeze(1), x_raw[a][:, :, BACK:T].unsqueeze(1))
-            for lo, hi, x_bf in ((HALF, BACK, front[:, HALF:BACK, :]), (0, HALF, front[:, 0:HALF, :]), (BACK, T, back[:])):
+            pieces = [(HALF, BACK, front[:, HALF:BACK, :]), (0, HALF, front[:, 0:HALF, :]), (BACK, T, back[:])]
+            if a < LAST:
+                shared_interleave(front[:].unsqueeze(1), x_raw[a][:, :, 0:BACK].unsqueeze(1), X_VECTOR[a])
+                interleave(nc.scalar.copy, back[:].unsqueeze(1), x_raw[a][:, :, BACK:T].unsqueeze(1))
+            else:
+                interleave(nc.scalar.copy, front[:, 0:HALF, :].unsqueeze(1), last_raw[0][:].unsqueeze(1))
+                shared_interleave(front[:, HALF:BACK, :].unsqueeze(1), last_raw[1][:, :, 0 : BACK - HALF].unsqueeze(1), X_VECTOR[a])
+                interleave(nc.scalar.copy, back[:].unsqueeze(1), last_raw[1][:, :, BACK - HALF : HALF].unsqueeze(1))
+                pieces = [pieces[1], pieces[0], pieces[2]]
+            for lo, hi, x_bf in pieces:
                 nc.vector.quantize_mx(
                     out=x_codes[a][:, lo:hi].bitcast(FP8X4),
                     scales=x_scales[4 * a : P, lo:hi],
                     in_=x_bf.rearrange("p t j -> p (t j)"),
                 )
             if a > 0:
-                gather_codes(a - 1, S - DEFERRED, S, picked_tile(a - 1, S - DEFERRED, S, f"x_raw{a}"))
+                gather_codes(a - 1, S - DEFERRED, S, picked_tile(a - 1, S - DEFERRED, S, f"x_raw{a}" if a < LAST else "last_raw1"))
             if a < LAST:
                 gather_codes(a, 0, S - DEFERRED, picked_tile(a, 0, S - DEFERRED, f"picked{a}"))
         nc.vector.tensor_copy(picked_scales[:], x_scales[:].indirect(offsets[:]))
@@ -151,13 +165,13 @@ def tile_picked_tome_lin_relu2_sub_e_kernel(tc, xT, w, b, gate, offs, out):
                 out=dst, in0=src.rearrange("p d j m -> p d m j"), scalar1=1.0, scalar2=0.0, op0=ALU.mult, op1=ALU.add
             )
 
-        gpsimd_interleave(first_bf[:], first_raw[:])
+        gpsimd_interleave(first_bf[:], first_raw[:, 0:ON_GPSIMD])
         for lo, hi in W_GROUPS:
             for m in range(max(lo, ON_GPSIMD), hi):
                 if m == SECOND:
-                    gpsimd_interleave(rounded(m, m + 1), w_raw[m][:].unsqueeze(1))
+                    gpsimd_interleave(rounded(m, m + 1), w_raw[m].unsqueeze(1))
                 else:
-                    interleave(nc.scalar.copy, rounded(m, m + 1), w_raw[m][:].unsqueeze(1))
+                    interleave(nc.scalar.copy, rounded(m, m + 1), w_raw[m].unsqueeze(1))
             nc.vector.quantize_mx(
                 out=w_codes[:, lo * N : hi * N].bitcast(FP8X4),
                 scales=w_scales(lo, hi),

@@ -20,22 +20,19 @@ PASS_K = P * PACK
 PASSES = K // PASS_K
 LAST = PASSES - 1
 HALF = T // 2
-X_WINDOW = 1408
-STORES = (384, 384, 256)
 VH = V // 2
 RUN = 4
+MATRICES = D * PASSES
+RAW = PACK * N * 4
 
 BACK = 768
 X_VECTOR = (512, 448, 400, 160)
 DEFERRED = 128
 CODE_WINDOW = 1216
-MATRICES = PASSES * D
-ON_GPSIMD = 3
-SECOND = 7
-W_GROUPS = ((0, 2), (2, 3), (3, 7), (8, 12), (7, 8), (12, 14), (14, 15), (15, 16))
-GATHER_AFTER = {6: (1, 3), 7: (3, 4)}
-RAW_AT = {6: 0, 7: 10240, 11: 12288}
-PICKED_AT = {6: 1024, 7: 11776}
+STORES = (256, 256, 256, 256)
+W_LOADS = ((0, 4), (4, 6), (6, 8), (8, 10), (10, 11), (11, 12), (12, 13), (13, 14), (14, 15), (15, 16))
+RAW_AT = {4: 0, 0: 2 * RAW, 6: 6 * RAW, 13: 8 * RAW, 8: 9 * RAW, 14: 11 * RAW}
+EARLY = 10
 
 
 def tile_picked_tome_lin_relu2_sub_e_kernel(tc, xT, w, b, gate, offs, out):
@@ -50,17 +47,14 @@ def tile_picked_tome_lin_relu2_sub_e_kernel(tc, xT, w, b, gate, offs, out):
         gates = keep.tile([P, S], F32, name="gates")
         x_raw = [keep.tile([P, PACK, T], F32, name=f"x_raw{a}", tag=f"x_raw{a}", align_bytes=64) for a in range(LAST)]
         last_raw = [keep.tile([P, PACK, HALF], F32, name=f"last_raw{c}", tag=f"last_raw{c}", align_bytes=64) for c in range(2)]
-        first_raw = reused.tile([P, D, PACK, N], F32, name="first_raw", align_bytes=64, offset=2048)
-        pair_raw = keep.tile([P, 2, PACK, N], F32, name="pair_raw", align_bytes=64)
-        w_raw = {ON_GPSIMD: first_raw[:, ON_GPSIMD], D: pair_raw[:, 0], D + 1: pair_raw[:, 1]}
-        for m in range(D + 2, MATRICES):
-            if m in RAW_AT:
-                w_raw[m] = reused.tile([P, PACK, N], F32, name=f"w_raw{m}", align_bytes=64, offset=RAW_AT[m])[:]
+        w_load = {}
+        for lo, hi in W_LOADS:
+            if lo in RAW_AT:
+                w_load[lo] = reused.tile([P, hi - lo, PACK, N], F32, name=f"w_raw{lo}", align_bytes=64, offset=RAW_AT[lo])
             else:
-                w_raw[m] = keep.tile([P, PACK, N], F32, name=f"w_raw{m}", tag=f"w_raw{m}", align_bytes=64)[:]
+                w_load[lo] = keep.tile([P, hi - lo, PACK, N], F32, name=f"w_raw{lo}", align_bytes=64)
         x_codes = [keep.tile([P, CODE_WINDOW if a < LAST else T], U32, name=f"x_codes{a}", align_bytes=64) for a in range(PASSES)]
-        x_scales = keep.tile([P, X_WINDOW], U8, name="x_scales", align_bytes=64)
-        picked_scales = keep.tile([P, S], U8, name="picked_scales", align_bytes=64)
+        x_scales = keep.tile([P, T], U8, name="x_scales", align_bytes=64)
         w_codes = keep.tile([P, MATRICES * N], U32, name="w_codes", align_bytes=64)
         windows = [keep.tile([P, T], F32, name=f"window{e}") for e in range(2)]
         acc = [psum.tile([P, VH], F32, name=f"acc{h}") for h in range(2)]
@@ -74,15 +68,13 @@ def tile_picked_tome_lin_relu2_sub_e_kernel(tc, xT, w, b, gate, offs, out):
                     nc.sync.dma_start(out=last_raw[c][:], in_=src[:, c * HALF : (c + 1) * HALF].rearrange("(p j) t -> p j t", j=PACK))
             if a == 0:
                 nc.sync.dma_start(offsets[:], offs)
-        nc.sync.dma_start(out=first_raw[:], in_=w[:, 0:PASS_K, :].rearrange("d (p j) m -> p d j m", j=PACK))
-        nc.sync.dma_start(out=pair_raw[:], in_=w[0:2, PASS_K : 2 * PASS_K, :].rearrange("d (p j) m -> p d j m", j=PACK))
-        for m in range(D + 2, MATRICES):
-            a, d = divmod(m, D)
-            src = w[d, a * PASS_K : (a + 1) * PASS_K, :]
-            nc.sync.dma_start(out=w_raw[m], in_=src.rearrange("(p j) m -> p j m", j=PACK))
+        for lo, hi in W_LOADS:
+            d, a = divmod(lo, PASSES)
+            src = w[d, a * PASS_K : (a + hi - lo) * PASS_K, :]
+            nc.sync.dma_start(out=w_load[lo][:], in_=src.rearrange("(a p j) m -> p a j m", p=P, j=PACK))
         nc.sync.dma_start(out=bias[:], in_=b)
-        for c in (1, 0):
-            nc.sync.dma_start(out=gates[:, c * HALF : (c + 1) * HALF], in_=gate[:, c * HALF : (c + 1) * HALF])
+        for lo, hi in ((HALF, HALF + VH), (HALF + VH, S), (0, HALF)):
+            nc.sync.dma_start(out=gates[:, lo:hi], in_=gate[:, lo:hi])
 
         nc.gpsimd.memset(x_scales[:], 0)
         for a in range(LAST):
@@ -98,21 +90,26 @@ def tile_picked_tome_lin_relu2_sub_e_kernel(tc, xT, w, b, gate, offs, out):
 
         def shared_interleave(dst, src, on_vector):
             width = dst.shape[2]
-            if on_vector > 0:
-                interleave(nc.vector.tensor_copy, dst[:, :, 0:on_vector, :], src[:, :, :, 0:on_vector])
-            if on_vector < width:
-                interleave(nc.scalar.copy, dst[:, :, on_vector:width, :], src[:, :, :, on_vector:width])
+            interleave(nc.vector.tensor_copy, dst[:, :, 0:on_vector, :], src[:, :, :, 0:on_vector])
+            interleave(nc.scalar.copy, dst[:, :, on_vector:width, :], src[:, :, :, on_vector:width])
 
         picked = {}
-
-        def picked_tile(a, lo, hi, tag):
-            return keep.tile([P, hi - lo], U32, name=f"picked{a}_{lo}", tag=tag, align_bytes=64)[:]
+        picked_scales = {}
 
         def gather_codes(a, lo, hi, dst):
             window = x_codes[a][:] if 4 * (hi - lo) > 3 * T else x_codes[a][:, 0:T]
-            nc.vector.tensor_copy(dst, window.indirect(offsets[:, lo // 16 : hi // 16]))
+            nc.vector.tensor_copy(dst[:], window.indirect(offsets[:, lo // 16 : hi // 16]))
             for s in range(lo, hi, VH):
                 picked[a, s] = dst[:, s - lo : s - lo + VH]
+
+        def gather_scales(lo, hi, dst):
+            nc.vector.tensor_copy(dst[:], x_scales[:].indirect(offsets[:, lo // 16 : hi // 16]))
+            for s in range(lo, hi, VH):
+                picked_scales[s] = (dst, s - lo)
+
+        def words(name, width, **where):
+            pool = reused if "offset" in where else keep
+            return pool.tile([P, width], U32, name=name, align_bytes=64, **where)
 
         for a in range(PASSES):
             front = keep.tile([P, BACK, PACK], BF16, name=f"x_front{a}", align_bytes=64)
@@ -133,79 +130,102 @@ def tile_picked_tome_lin_relu2_sub_e_kernel(tc, xT, w, b, gate, offs, out):
                     in_=x_bf.rearrange("p t j -> p (t j)"),
                 )
             if a > 0:
-                gather_codes(a - 1, S - DEFERRED, S, picked_tile(a - 1, S - DEFERRED, S, f"x_raw{a}" if a < LAST else "last_raw1"))
+                tag = f"x_raw{a}" if a < LAST else "last_raw1"
+                gather_codes(a - 1, S - DEFERRED, S, words(f"deferred{a}", DEFERRED, tag=tag))
             if a < LAST:
-                gather_codes(a, 0, S - DEFERRED, picked_tile(a, 0, S - DEFERRED, f"picked{a}"))
-        nc.vector.tensor_copy(picked_scales[:], x_scales[:].indirect(offsets[:]))
-        gather_codes(LAST, 0, V, picked_tile(LAST, 0, V, "picked_last0"))
+                gather_codes(a, 0, S - DEFERRED, words(f"picked{a}", S - DEFERRED))
+        gather_scales(0, HALF, keep.tile([P, HALF], U8, name="low_scales", align_bytes=64))
+        gather_codes(LAST, 0, V, words("last0", V))
 
-        early_scales = reused.tile([P, LAST * D * N], U8, name="early_scales", align_bytes=64, offset=3072)
-        late_scales = reused.tile([P, D * N], U8, name="late_scales", align_bytes=64, offset=RAW_AT[SECOND])
-
-        def w_scales(lo, hi):
-            if lo < LAST * D:
-                return early_scales[:, lo * N : hi * N]
-            return late_scales[:, (lo - LAST * D) * N : (hi - LAST * D) * N]
-
-        first_bf = keep.tile([P, ON_GPSIMD, N, PACK], BF16, name="first_bf", tag="ring", align_bytes=64)
+        early_scales = reused.tile([P, EARLY * N], U8, name="early_scales", align_bytes=64, offset=RAW_AT[0] + 5 * RAW // 4)
+        late_scales = reused.tile([P, (MATRICES - EARLY) * N], U8, name="late_scales", align_bytes=64, offset=RAW_AT[8] + RAW)
         w_bf = {
-            0: first_bf,
-            3: keep.tile([P, 4, N, PACK], BF16, name="w_bf3", tag="second_ring", align_bytes=64),
-            7: keep.tile([P, 1, N, PACK], BF16, name="w_bf7", tag="second_ring", align_bytes=64),
-            8: keep.tile([P, 4, N, PACK], BF16, name="w_bf8", align_bytes=64),
-            12: keep.tile([P, 4, N, PACK], BF16, name="w_bf12", align_bytes=64),
+            0: keep.tile([P, 4, N, PACK], BF16, name="w_bf0", tag="ring", align_bytes=64),
+            4: keep.tile([P, 2, N, PACK], BF16, name="w_bf4", tag="second_ring", align_bytes=64),
+            6: reused.tile([P, 2, N, PACK], BF16, name="w_bf6", align_bytes=64, offset=RAW_AT[0] + RAW // 4),
+            8: keep.tile([P, 2, N, PACK], BF16, name="w_bf8", tag="second_ring", align_bytes=64),
+            10: reused.tile([P, 6, N, PACK], BF16, name="w_bf10", align_bytes=64, offset=RAW_AT[0] + 2 * RAW),
         }
 
         def rounded(lo, hi):
             first = max(m for m in w_bf if m <= lo)
-            return w_bf[first][:, lo - first : hi - first, :, :]
+            return w_bf[first][:, lo - first : hi - first]
 
-        def gpsimd_interleave(dst, src):
+        def raw(lo, hi):
+            first = max(m for m in w_load if m <= lo)
+            return w_load[first][:, lo - first : hi - first]
+
+        def w_scales(lo, hi):
+            if lo < EARLY:
+                return early_scales[:, lo * N : hi * N]
+            return late_scales[:, (lo - EARLY) * N : (hi - EARLY) * N]
+
+        def round_on_gpsimd(lo, hi):
             nc.gpsimd.tensor_scalar(
-                out=dst, in0=src.rearrange("p d j m -> p d m j"), scalar1=1.0, scalar2=0.0, op0=ALU.mult, op1=ALU.add
+                out=rounded(lo, hi), in0=raw(lo, hi).rearrange("p d j m -> p d m j"), scalar1=1.0, scalar2=0.0, op0=ALU.mult, op1=ALU.add
             )
 
-        gpsimd_interleave(first_bf[:], first_raw[:, 0:ON_GPSIMD])
-        for lo, hi in W_GROUPS:
-            for m in range(max(lo, ON_GPSIMD), hi):
-                if m == SECOND:
-                    gpsimd_interleave(rounded(m, m + 1), w_raw[m].unsqueeze(1))
-                else:
-                    interleave(nc.scalar.copy, rounded(m, m + 1), w_raw[m].unsqueeze(1))
+        def round_on_scalar(lo, hi):
+            for m in range(lo, hi):
+                interleave(nc.scalar.copy, rounded(m, m + 1), raw(m, m + 1))
+
+        def quantise(lo, hi):
             nc.vector.quantize_mx(
                 out=w_codes[:, lo * N : hi * N].bitcast(FP8X4),
                 scales=w_scales(lo, hi),
                 in_=rounded(lo, hi).rearrange("p d m j -> p (d m j)"),
             )
-            if hi - 1 in GATHER_AFTER:
-                first, end = GATHER_AFTER[hi - 1]
-                if hi - 1 in PICKED_AT:
-                    dst = reused.tile([P, (end - first) * V], U32, name=f"picked_last{first}", align_bytes=64, offset=PICKED_AT[hi - 1])[:]
-                else:
-                    dst = picked_tile(LAST, first * V, end * V, f"w_raw{hi - 1}")
-                gather_codes(LAST, first * V, end * V, dst)
+
+        def multiply(lo, hi):
             for m in range(lo, hi):
-                a, d = divmod(m, D)
+                d, a = divmod(m, PASSES)
                 for h in range(2):
                     s = d * V + h * VH
+                    scales, at = picked_scales[s]
                     nc.tensor.matmul_mx(
                         out=acc[h][:],
                         lhsT=w_codes[:, m * N : (m + 1) * N].bitcast(FP8X4),
                         lhsT_scale=w_scales(m, m + 1),
                         rhs=picked[a, s].bitcast(FP8X4),
-                        rhs_scale=picked_scales[4 * a : P, s : s + VH],
+                        rhs_scale=scales[4 * a : P, at : at + VH],
                         start=(m == 0),
                         stop=(m == MATRICES - 1),
                     )
 
+        def step(lo, hi):
+            quantise(lo, hi)
+            multiply(lo, hi)
+
+        round_on_gpsimd(0, 2)
+        round_on_scalar(2, 4)
+        step(0, 4)
+        round_on_scalar(4, 6)
+        step(4, 6)
+        gather_scales(HALF, S, reused.tile([P, HALF], U8, name="high_scales", align_bytes=64, offset=RAW_AT[0] - HALF // 2))
+        round_on_gpsimd(8, 10)
+        round_on_scalar(6, 8)
+        gather_codes(LAST, V, 2 * V, words("last1", V, offset=RAW_AT[6] + 3 * RAW // 2))
+        step(6, 8)
+        step(8, 10)
+        gather_codes(LAST, 2 * V, 3 * V, words("last2", V, offset=RAW_AT[8] + RAW // 2))
+        round_on_scalar(10, 12)
+        step(10, 12)
+        round_on_scalar(12, 14)
+        step(12, 14)
+        gather_codes(LAST, 3 * V, S - VH, words("last3", VH, offset=RAW_AT[8] - RAW // 8))
+        round_on_scalar(14, 15)
+        step(14, 15)
+        gather_codes(LAST, S - VH, S, words("last4", VH, offset=RAW_AT[14] - RAW // 8))
+        round_on_scalar(15, 16)
+        step(15, 16)
+
         r = keep.tile([P, V], F32, name="r")
         y = keep.tile([P, 2 * V], F32, name="y")
-        weighted = keep.tile([P, S // 2], F32, name="weighted")
+        weighted = keep.tile([P, HALF], F32, name="weighted")
         lifted = keep.tile([P, VH], F32, name="lifted")
-        base = S // 2
         nc.vector.tensor_scalar(out=r[:, 0:VH], in0=acc[0][:], scalar1=bias[:, 0:1], scalar2=0.0, op0=ALU.add, op1=ALU.max)
         nc.vector.scalar_tensor_tensor(
-            out=lifted[:], in0=acc[0][:], scalar=bias[:, 0:1], in1=gates[:, base : base + VH], op0=ALU.add, op1=ALU.mult
+            out=lifted[:], in0=acc[0][:], scalar=bias[:, 0:1], in1=gates[:, HALF : HALF + VH], op0=ALU.add, op1=ALU.mult
         )
         nc.scalar.activation(out=r[:, VH:V], in_=acc[1][:], func=ACT.Relu, bias=bias[:, 0:1])
         nc.vector.tensor_tensor(weighted[:, 0:VH], r[:, 0:VH], lifted[:], ALU.mult)
@@ -213,12 +233,12 @@ def tile_picked_tome_lin_relu2_sub_e_kernel(tc, xT, w, b, gate, offs, out):
             nc.scalar.activation(out=y[:, h * VH : (h + 1) * VH], in_=r[:, h * VH : (h + 1) * VH], func=ACT.Square)
         nc.scalar.activation(out=y[:, V : 2 * V], in_=r[:], func=ACT.Square)
         for lo, hi in ((VH, V), (V, 2 * V)):
-            nc.vector.tensor_tensor(weighted[:, lo:hi], y[:, lo % V : lo % V + hi - lo], gates[:, base + lo : base + hi], ALU.mult)
-        for lo, hi in ((0, VH), (VH, 2 * V)):
+            nc.vector.tensor_tensor(weighted[:, lo:hi], y[:, lo % V : lo % V + hi - lo], gates[:, HALF + lo : HALF + hi], ALU.mult)
+        for lo, hi in ((0, VH), (VH, HALF)):
             nc.scalar.activation(
-                out=windows[1][:].indirect(offsets[:, (base + lo) // 16 : (base + hi) // 16]), in_=weighted[:, lo:hi], func=ACT.Copy
+                out=windows[1][:].indirect(offsets[:, (HALF + lo) // 16 : (HALF + hi) // 16]), in_=weighted[:, lo:hi], func=ACT.Copy
             )
-        nc.vector.tensor_tensor(windows[0][:].indirect(offsets[:, 0 : base // 16]), y[:], gates[:, 0:base], ALU.mult)
+        nc.vector.tensor_tensor(windows[0][:].indirect(offsets[:, 0 : HALF // 16]), y[:], gates[:, 0:HALF], ALU.mult)
         result = keep.tile([P, T], F32, name="result")
         lo = 0
         for width in STORES:

@@ -26,13 +26,15 @@ MATRICES = D * PASSES
 RAW = PACK * N * 4
 
 BACK = 768
-X_VECTOR = (512, 448, 400, 160)
+X_VECTOR = (512, 448, 128, 128)
+WHOLE = 2
 DEFERRED = 128
 CODE_WINDOW = 1216
 STORES = (256, 256, 256, 256)
 W_LOADS = ((0, 4), (4, 6), (6, 8), (8, 10), (10, 11), (11, 12), (12, 13), (13, 14), (14, 15), (15, 16))
 RAW_AT = {4: 0, 0: 2 * RAW, 6: 6 * RAW, 13: 8 * RAW, 8: 9 * RAW, 14: 11 * RAW}
 EARLY = 10
+WINDOW_WORDS = 384
 
 
 def tile_picked_tome_lin_relu2_sub_e_kernel(tc, xT, w, b, gate, offs, out):
@@ -45,8 +47,12 @@ def tile_picked_tome_lin_relu2_sub_e_kernel(tc, xT, w, b, gate, offs, out):
         offsets = keep.tile([P, S // 16], U16, name="offsets")
         bias = keep.tile([P, 1], F32, name="bias")
         gates = keep.tile([P, S], F32, name="gates")
-        x_raw = [keep.tile([P, PACK, T], F32, name=f"x_raw{a}", tag=f"x_raw{a}", align_bytes=64) for a in range(LAST)]
-        last_raw = [keep.tile([P, PACK, HALF], F32, name=f"last_raw{c}", tag=f"last_raw{c}", align_bytes=64) for c in range(2)]
+        x_raw = [keep.tile([P, PACK, T], F32, name=f"x_raw{a}", tag=f"x_raw{a}", align_bytes=64) for a in range(WHOLE)]
+        half_raw = {
+            (a, c): keep.tile([P, PACK, HALF], F32, name=f"half_raw{a}_{c}", tag=f"half_raw{a}_{c}", align_bytes=64)
+            for a in range(WHOLE, PASSES)
+            for c in range(2)
+        }
         w_load = {}
         for lo, hi in W_LOADS:
             if lo in RAW_AT:
@@ -61,11 +67,11 @@ def tile_picked_tome_lin_relu2_sub_e_kernel(tc, xT, w, b, gate, offs, out):
 
         for a in range(PASSES):
             src = xT[a * PASS_K : (a + 1) * PASS_K, :]
-            if a < LAST:
+            if a < WHOLE:
                 nc.sync.dma_start(out=x_raw[a][:], in_=src.rearrange("(p j) t -> p j t", j=PACK))
             else:
                 for c in range(2):
-                    nc.sync.dma_start(out=last_raw[c][:], in_=src[:, c * HALF : (c + 1) * HALF].rearrange("(p j) t -> p j t", j=PACK))
+                    nc.sync.dma_start(out=half_raw[a, c][:], in_=src[:, c * HALF : (c + 1) * HALF].rearrange("(p j) t -> p j t", j=PACK))
             if a == 0:
                 nc.sync.dma_start(offsets[:], offs)
         for lo, hi in W_LOADS:
@@ -73,7 +79,7 @@ def tile_picked_tome_lin_relu2_sub_e_kernel(tc, xT, w, b, gate, offs, out):
             src = w[d, a * PASS_K : (a + hi - lo) * PASS_K, :]
             nc.sync.dma_start(out=w_load[lo][:], in_=src.rearrange("(a p j) m -> p a j m", p=P, j=PACK))
         nc.sync.dma_start(out=bias[:], in_=b)
-        for lo, hi in ((HALF, HALF + VH), (HALF + VH, S), (0, HALF)):
+        for lo, hi in ((HALF, S), (0, HALF)):
             nc.sync.dma_start(out=gates[:, lo:hi], in_=gate[:, lo:hi])
 
         nc.gpsimd.memset(x_scales[:], 0)
@@ -115,13 +121,13 @@ def tile_picked_tome_lin_relu2_sub_e_kernel(tc, xT, w, b, gate, offs, out):
             front = keep.tile([P, BACK, PACK], BF16, name=f"x_front{a}", align_bytes=64)
             back = keep.tile([P, T - BACK, PACK], BF16, name=f"x_back{a}", tag="ring" if a == LAST else f"x_back{a}", align_bytes=64)
             pieces = [(HALF, BACK, front[:, HALF:BACK, :]), (0, HALF, front[:, 0:HALF, :]), (BACK, T, back[:])]
-            if a < LAST:
+            if a < WHOLE:
                 shared_interleave(front[:].unsqueeze(1), x_raw[a][:, :, 0:BACK].unsqueeze(1), X_VECTOR[a])
                 interleave(nc.scalar.copy, back[:].unsqueeze(1), x_raw[a][:, :, BACK:T].unsqueeze(1))
             else:
-                interleave(nc.scalar.copy, front[:, 0:HALF, :].unsqueeze(1), last_raw[0][:].unsqueeze(1))
-                shared_interleave(front[:, HALF:BACK, :].unsqueeze(1), last_raw[1][:, :, 0 : BACK - HALF].unsqueeze(1), X_VECTOR[a])
-                interleave(nc.scalar.copy, back[:].unsqueeze(1), last_raw[1][:, :, BACK - HALF : HALF].unsqueeze(1))
+                interleave(nc.scalar.copy, front[:, 0:HALF, :].unsqueeze(1), half_raw[a, 0][:].unsqueeze(1))
+                shared_interleave(front[:, HALF:BACK, :].unsqueeze(1), half_raw[a, 1][:, :, 0 : BACK - HALF].unsqueeze(1), X_VECTOR[a])
+                interleave(nc.scalar.copy, back[:].unsqueeze(1), half_raw[a, 1][:, :, BACK - HALF : HALF].unsqueeze(1))
                 pieces = [pieces[1], pieces[0], pieces[2]]
             for lo, hi, x_bf in pieces:
                 nc.vector.quantize_mx(
@@ -130,12 +136,12 @@ def tile_picked_tome_lin_relu2_sub_e_kernel(tc, xT, w, b, gate, offs, out):
                     in_=x_bf.rearrange("p t j -> p (t j)"),
                 )
             if a > 0:
-                tag = f"x_raw{a}" if a < LAST else "last_raw1"
+                tag = f"x_raw{a}" if a < WHOLE else f"half_raw{a}_1"
                 gather_codes(a - 1, S - DEFERRED, S, words(f"deferred{a}", DEFERRED, tag=tag))
             if a < LAST:
                 gather_codes(a, 0, S - DEFERRED, words(f"picked{a}", S - DEFERRED))
         gather_scales(0, HALF, keep.tile([P, HALF], U8, name="low_scales", align_bytes=64))
-        gather_codes(LAST, 0, V, words("last0", V))
+        gather_codes(LAST, 0, WINDOW_WORDS, words("last0", WINDOW_WORDS))
 
         early_scales = reused.tile([P, EARLY * N], U8, name="early_scales", align_bytes=64, offset=RAW_AT[0] + 5 * RAW // 4)
         late_scales = reused.tile([P, (MATRICES - EARLY) * N], U8, name="late_scales", align_bytes=64, offset=RAW_AT[8] + RAW)
@@ -204,10 +210,9 @@ def tile_picked_tome_lin_relu2_sub_e_kernel(tc, xT, w, b, gate, offs, out):
         gather_scales(HALF, S, reused.tile([P, HALF], U8, name="high_scales", align_bytes=64, offset=RAW_AT[0] - HALF // 2))
         round_on_gpsimd(8, 10)
         round_on_scalar(6, 8)
-        gather_codes(LAST, V, 2 * V, words("last1", V, offset=RAW_AT[6] + 3 * RAW // 2))
+        gather_codes(LAST, WINDOW_WORDS, 2 * WINDOW_WORDS, words("last1", WINDOW_WORDS, offset=RAW_AT[6] + 5 * RAW // 4))
         step(6, 8)
         step(8, 10)
-        gather_codes(LAST, 2 * V, 3 * V, words("last2", V, offset=RAW_AT[8] + RAW // 2))
         round_on_scalar(10, 12)
         step(10, 12)
         round_on_scalar(12, 14)

@@ -31,8 +31,8 @@ WHOLE = 2
 DEFERRED = 128
 CODE_WINDOW = 1216
 STORES = (256, 256, 256, 256)
-W_LOADS = ((0, 4), (4, 6), (6, 8), (8, 10), (10, 11), (11, 12), (12, 13), (13, 14), (14, 15), (15, 16))
-RAW_AT = {4: 0, 0: 2 * RAW, 6: 6 * RAW, 13: 8 * RAW, 8: 9 * RAW, 14: 11 * RAW}
+W_LOADS = ((0, 4), (4, 7), (7, 8), (8, 11), (11, 12), (12, 13), (13, 14), (14, 15), (15, 16))
+RAW_AT = {4: 0, 0: 3 * RAW, 7: 7 * RAW, 13: 8 * RAW, 8: 9 * RAW, 14: 12 * RAW}
 EARLY = 10
 WINDOW_WORDS = 384
 
@@ -79,7 +79,7 @@ def tile_picked_tome_lin_relu2_sub_e_kernel(tc, xT, w, b, gate, offs, out):
             src = w[d, a * PASS_K : (a + hi - lo) * PASS_K, :]
             nc.sync.dma_start(out=w_load[lo][:], in_=src.rearrange("(a p j) m -> p a j m", p=P, j=PACK))
         nc.sync.dma_start(out=bias[:], in_=b)
-        for lo, hi in ((HALF, S), (0, HALF)):
+        for lo, hi in ((HALF, HALF + VH), (HALF + VH, S), (0, HALF)):
             nc.sync.dma_start(out=gates[:, lo:hi], in_=gate[:, lo:hi])
 
         nc.gpsimd.memset(x_scales[:], 0)
@@ -143,14 +143,15 @@ def tile_picked_tome_lin_relu2_sub_e_kernel(tc, xT, w, b, gate, offs, out):
         gather_scales(0, HALF, keep.tile([P, HALF], U8, name="low_scales", align_bytes=64))
         gather_codes(LAST, 0, WINDOW_WORDS, words("last0", WINDOW_WORDS))
 
-        early_scales = reused.tile([P, EARLY * N], U8, name="early_scales", align_bytes=64, offset=RAW_AT[0] + 5 * RAW // 4)
+        early_scales = reused.tile([P, EARLY * N], U8, name="early_scales", align_bytes=64, offset=RAW_AT[0] + 5 * RAW // 8)
         late_scales = reused.tile([P, (MATRICES - EARLY) * N], U8, name="late_scales", align_bytes=64, offset=RAW_AT[8] + RAW)
         w_bf = {
             0: keep.tile([P, 4, N, PACK], BF16, name="w_bf0", tag="ring", align_bytes=64),
-            4: keep.tile([P, 2, N, PACK], BF16, name="w_bf4", tag="second_ring", align_bytes=64),
-            6: reused.tile([P, 2, N, PACK], BF16, name="w_bf6", align_bytes=64, offset=RAW_AT[0] + RAW // 4),
+            4: keep.tile([P, 2, N, PACK], BF16, name="w_bf4", align_bytes=64),
+            6: keep.tile([P, 1, N, PACK], BF16, name="w_bf6", tag="second_ring", align_bytes=64),
+            7: reused.tile([P, 1, N, PACK], BF16, name="w_bf7", align_bytes=64, offset=RAW_AT[0] + RAW // 8),
             8: keep.tile([P, 2, N, PACK], BF16, name="w_bf8", tag="second_ring", align_bytes=64),
-            10: reused.tile([P, 6, N, PACK], BF16, name="w_bf10", align_bytes=64, offset=RAW_AT[0] + 2 * RAW),
+            10: reused.tile([P, 6, N, PACK], BF16, name="w_bf10", align_bytes=64, offset=RAW_AT[0] + 5 * RAW // 4),
         }
 
         def rounded(lo, hi):
@@ -207,11 +208,13 @@ def tile_picked_tome_lin_relu2_sub_e_kernel(tc, xT, w, b, gate, offs, out):
         step(0, 4)
         round_on_scalar(4, 6)
         step(4, 6)
+        round_on_scalar(6, 7)
+        step(6, 7)
         gather_scales(HALF, S, reused.tile([P, HALF], U8, name="high_scales", align_bytes=64, offset=RAW_AT[0] - HALF // 2))
         round_on_gpsimd(8, 10)
-        round_on_scalar(6, 8)
-        gather_codes(LAST, WINDOW_WORDS, 2 * WINDOW_WORDS, words("last1", WINDOW_WORDS, offset=RAW_AT[6] + 5 * RAW // 4))
-        step(6, 8)
+        round_on_scalar(7, 8)
+        gather_codes(LAST, WINDOW_WORDS, 2 * WINDOW_WORDS, words("last1", WINDOW_WORDS, offset=RAW_AT[7] + RAW // 4))
+        step(7, 8)
         step(8, 10)
         round_on_scalar(10, 12)
         step(10, 12)

from contextlib import ExitStack

import concourse.mybir as mybir

K, T, D, S, V, N = 2048, 1024, 4, 1024, 256, 128
FLOPS = 2 * N * S * K

F32 = mybir.dt.float32
BF16 = mybir.dt.bfloat16
U32 = mybir.dt.uint32
U16 = mybir.dt.uint16
U8 = mybir.dt.uint8
FP8X4 = mybir.dt.float8_e4m3fn_x4
ACT = mybir.ActivationFunctionType
ALU = mybir.AluOpType

P = 128
PACK = 4
PASS_K = P * PACK
PASSES = K // PASS_K
LAST = PASSES - 1
HALF = T // 2
VH = V // 2
RUN = 4
MATRICES = D * PASSES
RAW = PACK * N * 4

BACK = 768
X_VECTOR = (512, 448, 128, 128)
WHOLE = 2
DEFERRED = 128
CODE_WINDOW = 1216
STORES = (256, 256, 256, 256)
W_LOADS = ((0, 4), (4, 7), (7, 8), (8, 11), (11, 12), (12, 13), (13, 14), (14, 15), (15, 16))
RAW_AT = {4: 0, 0: 3 * RAW, 7: 7 * RAW, 13: 8 * RAW, 8: 9 * RAW, 14: 12 * RAW}
EARLY = 10
WINDOW_WORDS = 384


def tile_picked_tome_lin_relu2_sub_e_kernel(tc, xT, w, b, gate, offs, out):
    nc = tc.nc
    with ExitStack() as ctx:
        keep = ctx.enter_context(tc.tile_pool(name="keep", bufs=1))
        reused = ctx.enter_context(tc.tile_pool(name="reused", bufs=1))
        psum = ctx.enter_context(tc.psum_pool(name="psum", bufs=1))

        offsets = keep.tile([P, S // 16], U16, name="offsets")
        bias = keep.tile([P, 1], F32, name="bias")
        gates = keep.tile([P, S], F32, name="gates")
        x_raw = [keep.tile([P, PACK, T], F32, name=f"x_raw{a}", tag=f"x_raw{a}", align_bytes=64) for a in range(WHOLE)]
        half_raw = {
            (a, c): keep.tile([P, PACK, HALF], F32, name=f"half_raw{a}_{c}", tag=f"half_raw{a}_{c}", align_bytes=64)
            for a in range(WHOLE, PASSES)
            for c in range(2)
        }
        w_load = {}
        for lo, hi in W_LOADS:
            if lo in RAW_AT:
                w_load[lo] = reused.tile([P, hi - lo, PACK, N], F32, name=f"w_raw{lo}", align_bytes=64, offset=RAW_AT[lo])
            else:
                w_load[lo] = keep.tile([P, hi - lo, PACK, N], F32, name=f"w_raw{lo}", align_bytes=64)
        x_codes = [keep.tile([P, CODE_WINDOW if a < LAST else T], U32, name=f"x_codes{a}", align_bytes=64) for a in range(PASSES)]
        x_scales = keep.tile([P, T], U8, name="x_scales", align_bytes=64)
        w_codes = keep.tile([P, MATRICES * N], U32, name="w_codes", align_bytes=64)
        windows = [keep.tile([P, T], F32, name=f"window{e}") for e in range(2)]
        acc = [psum.tile([P, VH], F32, name=f"acc{h}") for h in range(2)]

        for a in range(PASSES):
            src = xT[a * PASS_K : (a + 1) * PASS_K, :]
            if a < WHOLE:
                nc.sync.dma_start(out=x_raw[a][:], in_=src.rearrange("(p j) t -> p j t", j=PACK))
            else:
                for c in range(2):
                    nc.sync.dma_start(out=half_raw[a, c][:], in_=src[:, c * HALF : (c + 1) * HALF].rearrange("(p j) t -> p j t", j=PACK))
            if a == 0:
                nc.sync.dma_start(offsets[:], offs)
        for lo, hi in W_LOADS:
            d, a = divmod(lo, PASSES)
            src = w[d, a * PASS_K : (a + hi - lo) * PASS_K, :]
            nc.sync.dma_start(out=w_load[lo][:], in_=src.rearrange("(a p j) m -> p a j m", p=P, j=PACK))
        nc.sync.dma_start(out=bias[:], in_=b)
        for lo, hi in ((HALF, HALF + VH), (HALF + VH, S), (0, HALF)):
            nc.sync.dma_start(out=gates[:, lo:hi], in_=gate[:, lo:hi])

        nc.gpsimd.memset(x_scales[:], 0)
        for a in range(LAST):
            nc.gpsimd.memset(x_codes[a][:, T:CODE_WINDOW], 0)
        for window in windows:
            nc.gpsimd.memset(window[:], 0.0)

        def interleave(copy, dst, src):
            copy(
                out=dst.rearrange("p d (c i) j -> p d c j i", i=RUN),
                in_=src.rearrange("p d j (c i) -> p d c j i", i=RUN),
            )

        def shared_interleave(dst, src, on_vector):
            width = dst.shape[2]
            interleave(nc.vector.tensor_copy, dst[:, :, 0:on_vector, :], src[:, :, :, 0:on_vector])
            interleave(nc.scalar.copy, dst[:, :, on_vector:width, :], src[:, :, :, on_vector:width])

        picked = {}
        picked_scales = {}

        def gather_codes(a, lo, hi, dst):
            window = x_codes[a][:] if 4 * (hi - lo) > 3 * T else x_codes[a][:, 0:T]
            nc.vector.tensor_copy(dst[:], window.indirect(offsets[:, lo // 16 : hi // 16]))
            for s in range(lo, hi, VH):
                picked[a, s] = dst[:, s - lo : s - lo + VH]

        def gather_scales(lo, hi, dst):
            nc.vector.tensor_copy(dst[:], x_scales[:].indirect(offsets[:, lo // 16 : hi // 16]))
            for s in range(lo, hi, VH):
                picked_scales[s] = (dst, s - lo)

        def words(name, width, **where):
            pool = reused if "offset" in where else keep
            return pool.tile([P, width], U32, name=name, align_bytes=64, **where)

        for a in range(PASSES):
            front = keep.tile([P, BACK, PACK], BF16, name=f"x_front{a}", align_bytes=64)
            back = keep.tile([P, T - BACK, PACK], BF16, name=f"x_back{a}", tag="ring" if a == LAST else f"x_back{a}", align_bytes=64)
            pieces = [(HALF, BACK, front[:, HALF:BACK, :]), (0, HALF, front[:, 0:HALF, :]), (BACK, T, back[:])]
            if a < WHOLE:
                shared_interleave(front[:].unsqueeze(1), x_raw[a][:, :, 0:BACK].unsqueeze(1), X_VECTOR[a])
                interleave(nc.scalar.copy, back[:].unsqueeze(1), x_raw[a][:, :, BACK:T].unsqueeze(1))
            else:
                interleave(nc.scalar.copy, front[:, 0:HALF, :].unsqueeze(1), half_raw[a, 0][:].unsqueeze(1))
                shared_interleave(front[:, HALF:BACK, :].unsqueeze(1), half_raw[a, 1][:, :, 0 : BACK - HALF].unsqueeze(1), X_VECTOR[a])
                interleave(nc.scalar.copy, back[:].unsqueeze(1), half_raw[a, 1][:, :, BACK - HALF : HALF].unsqueeze(1))
                pieces = [pieces[1], pieces[0], pieces[2]]
            for lo, hi, x_bf in pieces:
                nc.vector.quantize_mx(
                    out=x_codes[a][:, lo:hi].bitcast(FP8X4),
                    scales=x_scales[4 * a : P, lo:hi],
                    in_=x_bf.rearrange("p t j -> p (t j)"),
                )
            if a > 0:
                tag = f"x_raw{a}" if a < WHOLE else f"half_raw{a}_1"
                gather_codes(a - 1, S - DEFERRED, S, words(f"deferred{a}", DEFERRED, tag=tag))
            if a < LAST:
                gather_codes(a, 0, S - DEFERRED, words(f"picked{a}", S - DEFERRED))
        gather_scales(0, HALF, keep.tile([P, HALF], U8, name="low_scales", align_bytes=64))
        gather_codes(LAST, 0, WINDOW_WORDS, words("last0", WINDOW_WORDS))

        early_scales = reused.tile([P, EARLY * N], U8, name="early_scales", align_bytes=64, offset=RAW_AT[0] + 5 * RAW // 8)
        late_scales = reused.tile([P, (MATRICES - EARLY) * N], U8, name="late_scales", align_bytes=64, offset=RAW_AT[8] + RAW)
        w_bf = {
            0: keep.tile([P, 4, N, PACK], BF16, name="w_bf0", tag="ring", align_bytes=64),
            4: keep.tile([P, 2, N, PACK], BF16, name="w_bf4", align_bytes=64),
            6: keep.tile([P, 1, N, PACK], BF16, name="w_bf6", tag="second_ring", align_bytes=64),
            7: reused.tile([P, 1, N, PACK], BF16, name="w_bf7", align_bytes=64, offset=RAW_AT[0] + RAW // 8),
            8: keep.tile([P, 2, N, PACK], BF16, name="w_bf8", tag="second_ring", align_bytes=64),
            10: reused.tile([P, 6, N, PACK], BF16, name="w_bf10", align_bytes=64, offset=RAW_AT[0] + 5 * RAW // 4),
        }

        def rounded(lo, hi):
            first = max(m for m in w_bf if m <= lo)
            return w_bf[first][:, lo - first : hi - first]

        def raw(lo, hi):
            first = max(m for m in w_load if m <= lo)
            return w_load[first][:, lo - first : hi - first]

        def w_scales(lo, hi):
            if lo < EARLY:
                return early_scales[:, lo * N : hi * N]
            return late_scales[:, (lo - EARLY) * N : (hi - EARLY) * N]

        def round_on_gpsimd(lo, hi):
            nc.gpsimd.tensor_scalar(
                out=rounded(lo, hi), in0=raw(lo, hi).rearrange("p d j m -> p d m j"), scalar1=1.0, scalar2=0.0, op0=ALU.mult, op1=ALU.add
            )

        def round_on_scalar(lo, hi):
            for m in range(lo, hi):
                interleave(nc.scalar.copy, rounded(m, m + 1), raw(m, m + 1))

        def quantise(lo, hi):
            nc.vector.quantize_mx(
                out=w_codes[:, lo * N : hi * N].bitcast(FP8X4),
                scales=w_scales(lo, hi),
                in_=rounded(lo, hi).rearrange("p d m j -> p (d m j)"),
            )

        def multiply(lo, hi):
            for m in range(lo, hi):
                d, a = divmod(m, PASSES)
                for h in range(2):
                    s = d * V + h * VH
                    scales, at = picked_scales[s]
                    nc.tensor.matmul_mx(
                        out=acc[h][:],
                        lhsT=w_codes[:, m * N : (m + 1) * N].bitcast(FP8X4),
                        lhsT_scale=w_scales(m, m + 1),
                        rhs=picked[a, s].bitcast(FP8X4),
                        rhs_scale=scales[4 * a : P, at : at + VH],
                        start=(m == 0),
                        stop=(m == MATRICES - 1),
                    )

        def step(lo, hi):
            quantise(lo, hi)
            multiply(lo, hi)

        round_on_gpsimd(0, 2)
        round_on_scalar(2, 4)
        step(0, 4)
        round_on_scalar(4, 6)
        step(4, 6)
        round_on_scalar(6, 7)
        step(6, 7)
        gather_scales(HALF, S, reused.tile([P, HALF], U8, name="high_scales", align_bytes=64, offset=RAW_AT[0] - HALF // 2))
        round_on_gpsimd(8, 10)
        round_on_scalar(7, 8)
        gather_codes(LAST, WINDOW_WORDS, 2 * WINDOW_WORDS, words("last1", WINDOW_WORDS, offset=RAW_AT[7] + RAW // 4))
        step(7, 8)
        step(8, 10)
        round_on_scalar(10, 12)
        step(10, 12)
        round_on_scalar(12, 14)
        step(12, 14)
        gather_codes(LAST, 3 * V, S - VH, words("last3", VH, offset=RAW_AT[8] - RAW // 8))
        round_on_scalar(14, 15)
        step(14, 15)
        gather_codes(LAST, S - VH, S, words("last4", VH, offset=RAW_AT[14] - RAW // 8))
        round_on_scalar(15, 16)
        step(15, 16)

        r = keep.tile([P, V], F32, name="r")
        y = keep.tile([P, 2 * V], F32, name="y")
        weighted = keep.tile([P, HALF], F32, name="weighted")
        lifted = keep.tile([P, VH], F32, name="lifted")
        nc.vector.tensor_scalar(out=r[:, 0:VH], in0=acc[0][:], scalar1=bias[:, 0:1], scalar2=0.0, op0=ALU.add, op1=ALU.max)
        nc.vector.scalar_tensor_tensor(
            out=lifted[:], in0=acc[0][:], scalar=bias[:, 0:1], in1=gates[:, HALF : HALF + VH], op0=ALU.add, op1=ALU.mult
        )
        nc.scalar.activation(out=r[:, VH:V], in_=acc[1][:], func=ACT.Relu, bias=bias[:, 0:1])
        nc.vector.tensor_tensor(weighted[:, 0:VH], r[:, 0:VH], lifted[:], ALU.mult)
        for h in (1, 0):
            nc.scalar.activation(out=y[:, h * VH : (h + 1) * VH], in_=r[:, h * VH : (h + 1) * VH], func=ACT.Square)
        nc.scalar.activation(out=y[:, V : 2 * V], in_=r[:], func=ACT.Square)
        for lo, hi in ((VH, V), (V, 2 * V)):
            nc.vector.tensor_tensor(weighted[:, lo:hi], y[:, lo % V : lo % V + hi - lo], gates[:, HALF + lo : HALF + hi], ALU.mult)
        for lo, hi in ((0, VH), (VH, HALF)):
            nc.scalar.activation(
                out=windows[1][:].indirect(offsets[:, (HALF + lo) // 16 : (HALF + hi) // 16]), in_=weighted[:, lo:hi], func=ACT.Copy
            )
        nc.vector.tensor_tensor(windows[0][:].indirect(offsets[:, 0 : HALF // 16]), y[:], gates[:, 0:HALF], ALU.mult)
        result = keep.tile([P, T], F32, name="result")
        lo = 0
        for width in STORES:
            cols = slice(lo, lo + width)
            nc.vector.tensor_tensor(result[:, cols], windows[0][:, cols], windows[1][:, cols], ALU.add)
            nc.sync.dma_start(out=out[:, cols], in_=result[:, cols])
            lo = lo + width
